import numpy as np
import ml_dtypes


def mxq(x, axis, fmt="e4m3"):
    dtype, down = {"e4m3": (ml_dtypes.float8_e4m3fn, 7), "e5m2": (ml_dtypes.float8_e5m2, 14)}[fmt]
    v = np.moveaxis(np.asarray(x, np.float32).astype(ml_dtypes.bfloat16).astype(np.float64), axis, -1)
    blocks = v.reshape(v.shape[:-1] + (-1, 32))
    amax = np.abs(blocks).max(-1, keepdims=True)
    byte = np.maximum(np.where(amax > 0, np.frexp(amax)[1] - 1 + 127, 0) - down, 1)
    scale = np.exp2(byte - 127.0)
    codes = (blocks / scale).astype(np.float32).astype(dtype).astype(np.float64)
    return np.moveaxis((codes * scale).reshape(v.shape), -1, axis)


WIDE = False


def mx_kscale(k):
    if not WIDE:
        return np.ones(k)
    levels = np.array([10, -10, 5, -5, 0])
    if k % 512:
        return np.exp2(np.random.permutation(np.resize(levels, k // 32))).repeat(32)
    a = np.empty((k // 512, 16))
    for p in range(k // 512):
        a[p, :8] = np.random.permutation(np.resize(levels, 8))
        for g in range(8):
            far = levels[np.abs(levels - a[p, g]) >= 10]
            a[p, g + 8] = far[np.random.randint(len(far))]
    return np.exp2(a.ravel()).repeat(32)


def f64(x):
    return np.asarray(x).astype(np.float64)


def striped(idx):
    return np.tile(np.asarray(idx).reshape(-1, 16).T, (8, 1)).astype(np.uint16)


def unstriped(offs):
    return offs[:16].T.reshape(-1).astype(np.int64)


E2M1 = np.array([0.0, 0.5, 1.0, 1.5, 2.0, 3.0, 4.0, 6.0, -0.0, -0.5, -1.0, -1.5, -2.0, -3.0, -4.0, -6.0])


def pack_weight(w, fmt):
    k, n = w.shape
    w = f64(np.asarray(w, np.float32).astype(ml_dtypes.bfloat16)).reshape(k // 32, 32, n)
    amax = np.abs(w).max(1)
    if fmt == "e4m3":
        byte = np.frexp(amax)[1] - 1 + 127 - 7
    else:
        mant, ex = np.frexp(amax / 6.0)
        byte = np.where(mant > 0.5, ex, ex - 1) + 127
    byte = np.clip(np.where(amax > 0, byte, 1), 1, 254)
    scaled = (w * np.exp2(127.0 - byte)[:, None, :]).reshape(k, n).astype(np.float32)
    by_word = np.ascontiguousarray(scaled.reshape(k // 512, 128, 4, n).transpose(0, 1, 3, 2))
    if fmt == "e4m3":
        words = by_word.astype(ml_dtypes.float8_e4m3fn).view(np.uint8)
    else:
        c = by_word.astype(ml_dtypes.float4_e2m1fn).view(np.uint8) & 0xF
        words = (c[..., 0::2] | (c[..., 1::2] << 4)).reshape(k // 512, 128, 2 * n)
    return np.ascontiguousarray(words), np.ascontiguousarray(byte.astype(np.uint8).reshape(k // 512, 16, n))


def unpack_weight(words, scales, fmt):
    g, _, n = scales.shape
    words = np.ascontiguousarray(words).reshape(g, 128, n, -1)
    if fmt == "e4m3":
        vals = words.view(ml_dtypes.float8_e4m3fn).astype(np.float64)
    else:
        nib = np.empty((g, 128, n, 4), np.uint8)
        nib[..., 0::2] = words & 0xF
        nib[..., 1::2] = words >> 4
        vals = E2M1[nib]
    vals = vals * np.repeat(np.exp2(scales.astype(np.float64) - 127.0), 8, axis=1)[..., None]
    return vals.transpose(0, 1, 3, 2).reshape(g * 512, n)


B, N, T, D, NQ = 1, 512, 2048, 1024, 128


def setup_inputs():
    n = np.random.standard_normal
    idx = np.random.permutation(T)[:B * N]
    s = mx_kscale(D)[:, None]
    kp = pack_weight(n((D, T)) / s, "e2m1")
    return {
        "qT": (n((B, D, NQ)) * s * (1.00 / np.sqrt(D))).astype(np.float32),
        "k_words": np.ascontiguousarray(kp[0].reshape(1, 2, 128, T, 2).transpose(0, 2, 3, 1, 4)).reshape(1, 128, T, 4),
        "k_scales": kp[1],
        "offs": striped(idx),
    }


def reference(qT, k_words, k_scales, offs):
    idx = unstriped(offs)
    pick = lambda x, which: x[:, which].reshape(x.shape[0], B, -1).transpose(1, 0, 2)
    k = unpack_weight(k_words.reshape(1, 128, T, 2, 2).transpose(0, 3, 1, 2, 4).reshape(2, 128, 2 * T), k_scales, "e2m1")
    kg = pick(k, idx)
    qq = mxq(f64(qT), 1, "e4m3")
    a = qq.transpose(0, 2, 1) @ kg
    lo = np.min(a, axis=-1, keepdims=True)
    hi = np.max(a, axis=-1, keepdims=True)
    y = (a - lo) / (hi - lo)
    return y

@@ -1,0 +1,114 @@
+from contextlib import ExitStack
+
+import concourse.mybir as mybir
+
+F32 = mybir.dt.float32
+BF16 = mybir.dt.bfloat16
+I32 = mybir.dt.int32
+U32 = mybir.dt.uint32
+U16 = mybir.dt.uint16
+U8 = mybir.dt.uint8
+FP8X4 = mybir.dt.float8_e4m3fn_x4
+FP4X4 = mybir.dt.float4_e2m1fn_x4
+ALU = mybir.AluOpType
+
+P = 128
+PACK = 4
+PASSES = 2
+T = 2048
+N = 512
+NQ = 128
+HALF = N // 2
+GROUP = 128
+
+FLOPS = 2 * NQ * N * PASSES * P * PACK
+
+
+def tile_attend_nrm_minmax_topk_kernel(tc, qT, k_words, k_scales, offs, out):
+    nc = tc.nc
+    with ExitStack() as ctx:
+        sb = ctx.enter_context(tc.tile_pool(name="sb", bufs=1))
+        psum = ctx.enter_context(tc.psum_pool(name="psum", bufs=1))
+
+        offsets = sb.tile([P, N // 16], U16, name="offsets")
+        scale_pool = sb.tile([P, T], U8, name="scale_pool", align_bytes=64)
+        planes = sb.tile([P, PASSES, N], U8, name="planes", align_bytes=64)
+        word_pool = sb.tile([P, T], I32, name="word_pool", align_bytes=64)
+        q_raw = [sb.tile([P, PACK, NQ], F32, name=f"q_raw{o}") for o in range(PASSES)]
+
+        nc.vector.memset(scale_pool[:].bitcast(I32), 0)
+        nc.vector.memset(planes[:].rearrange("p o n -> p (o n)").bitcast(I32), 0)
+
+        q_rows = qT[0].rearrange("(o p j) w -> o p j w", o=PASSES, j=PACK)
+        nc.sync.dma_start(offsets[:], offs)
+        nc.sync.dma_start(out=q_raw[0][:], in_=q_rows[0])
+        nc.sync.dma_start(
+            out=scale_pool[0:P:4, :].bitcast(I32),
+            in_=k_scales.rearrange("o f t -> (o f) t").bitcast(I32),
+        )
+        nc.sync.dma_start(out=q_raw[1][:], in_=q_rows[1])
+        nc.sync.dma_start(out=word_pool[:], in_=k_words[0].rearrange("p t b -> p (t b)").bitcast(I32))
+
+        picked_scales = sb.tile([P, N], U8, name="picked_scales", align_bytes=64)
+        nc.vector.tensor_copy(picked_scales[:], scale_pool[:].indirect(offsets[:]))
+        for o in range(PASSES):
+            for r in range(4):
+                nc.sync.dma_start(
+                    out=planes[r:P:32, o, :].bitcast(I32),
+                    in_=picked_scales[64 * o + 4 * r : 64 * (o + 1) : 16, :].bitcast(I32),
+                )
+
+        q_codes = sb.tile([P, PASSES, NQ], U32, name="q_codes", align_bytes=64)
+        q_scales = sb.tile([P, PASSES, NQ], U8, name="q_scales", align_bytes=64)
+        q_grouped = sb.tile([P, PASSES, NQ, PACK], BF16, name="q_grouped", align_bytes=64)
+        for o in range(PASSES):
+            nc.scalar.copy(out=q_grouped[:, o], in_=q_raw[o][:].rearrange("p j w -> p w j"))
+        nc.vector.quantize_mx(
+            out=q_codes[:].rearrange("p o w -> p (o w)").bitcast(FP8X4),
+            scales=q_scales[:].rearrange("p o w -> p (o w)"),
+            in_=q_grouped[:].rearrange("p o w j -> p (o w j)"),
+        )
+
+        banks = []
+        for h in range(2):
+            picked = sb.tile([P, HALF], U32, name=f"picked{h}", align_bytes=64)
+            nc.vector.tensor_copy(
+                picked[:], word_pool[:].bitcast(U32).indirect(offsets[:, h * HALF // 16 : (h + 1) * HALF // 16])
+            )
+            keys = sb.tile([P, PASSES, HALF], U16, name=f"keys{h}", align_bytes=64)
+            nc.vector.tensor_copy(keys[:], picked[:].bitcast(U16).rearrange("p (n o) -> p o n", o=PASSES))
+            bank = psum.tile([P, HALF], F32, name=f"bank{h}")
+            for g in range(HALF // GROUP):
+                cols = slice(g * GROUP, (g + 1) * GROUP)
+                slots = slice(h * HALF + g * GROUP, h * HALF + (g + 1) * GROUP)
+                for o in range(PASSES):
+                    nc.tensor.matmul_mx(
+                        out=bank[:, cols],
+                        lhsT=q_codes[:, o, :].bitcast(FP8X4),
+                        lhsT_scale=q_scales[:, o, :],
+                        rhs=keys[:, o, cols].bitcast(FP4X4),
+                        rhs_scale=planes[:, o, slots],
+                        start=(o == 0),
+                        stop=(o == PASSES - 1),
+                    )
+            banks.append(bank)
+
+        hi = [sb.tile([P, 1], F32, name=f"hi{h}") for h in range(2)]
+        lo = [sb.tile([P, 1], F32, name=f"lo{h}") for h in range(2)]
+        scores = [sb.tile([P, HALF], F32, name=f"scores{h}") for h in range(2)]
+        spare = [sb.tile([P, HALF], F32, name=f"spare{h}") for h in range(2)]
+        for h in range(2):
+            nc.vector.tensor_scalar(
+                scores[h][:], banks[h][:], 1.0, hi[0][:] if h else None, ALU.mult, ALU.max, accum_out=hi[h][:]
+            )
+            nc.vector.tensor_scalar(
+                spare[h][:], banks[h][:], 1.0, lo[0][:] if h else None, ALU.mult, ALU.min, accum_out=lo[h][:]
+            )
+        span = sb.tile([P, 1], F32, name="span")
+        inv_span = sb.tile([P, 1], F32, name="inv_span")
+        nc.vector.tensor_tensor(span[:], hi[1][:], lo[1][:], ALU.subtract)
+        nc.vector.reciprocal(inv_span[:], span[:])
+        for h, queue in enumerate((nc.sync, nc.scalar)):
+            result = sb.tile([P, HALF], F32, name=f"result{h}")
+            nc.vector.tensor_scalar(result[:], scores[h][:], lo[1][:], inv_span[:], ALU.subtract, ALU.mult)
+            queue.dma_start(out=out[0, :, h * HALF : (h + 1) * HALF], in_=result[:])

@@ -40,43 +40,51 @@ def tile_attend_nrm_minmax_topk_kernel(tc, qT, k_words, k_scales, offs, out):
         nc.vector.memset(planes[:].rearrange("p o n -> p (o n)").bitcast(I32), 0)
 
         q_rows = qT[0].rearrange("(o p j) w -> o p j w", o=PASSES, j=PACK)
+        nc.scalar.dma_start(out=word_pool[:], in_=k_words[0].rearrange("p t b -> p (t b)").bitcast(I32))
+        for o in range(PASSES):
+            nc.scalar.dma_start(out=q_raw[o][:], in_=q_rows[o])
         nc.sync.dma_start(offsets[:], offs)
-        nc.sync.dma_start(out=q_raw[0][:], in_=q_rows[0])
         nc.sync.dma_start(
             out=scale_pool[0:P:4, :].bitcast(I32),
-            in_=k_scales.rearrange("o f t -> (o f) t").bitcast(I32),
+            in_=k_scales.rearrange("o f t -> f o t").bitcast(I32),
         )
-        nc.sync.dma_start(out=q_raw[1][:], in_=q_rows[1])
-        nc.sync.dma_start(out=word_pool[:], in_=k_words[0].rearrange("p t b -> p (t b)").bitcast(I32))
 
         picked_scales = sb.tile([P, N], U8, name="picked_scales", align_bytes=64)
         nc.vector.tensor_copy(picked_scales[:], scale_pool[:].indirect(offsets[:]))
-        for o in range(PASSES):
-            for r in range(4):
-                nc.sync.dma_start(
-                    out=planes[r:P:32, o, :].bitcast(I32),
-                    in_=picked_scales[64 * o + 4 * r : 64 * (o + 1) : 16, :].bitcast(I32),
-                )
+        for quad in range(0, P, 32):
+            nc.sync.dma_start(
+                out=planes[quad : quad + 4].rearrange("p o n -> p (o n)").bitcast(I32),
+                in_=picked_scales[quad : quad + 32 : 4, :].bitcast(I32),
+            )
 
-        q_codes = sb.tile([P, PASSES, NQ], U32, name="q_codes", align_bytes=64)
-        q_scales = sb.tile([P, PASSES, NQ], U8, name="q_scales", align_bytes=64)
-        q_grouped = sb.tile([P, PASSES, NQ, PACK], BF16, name="q_grouped", align_bytes=64)
+        picked = [sb.tile([P, HALF], U32, name=f"picked{h}", align_bytes=64) for h in range(2)]
+        keys = [sb.tile([P, PASSES, HALF], U16, name=f"keys{h}", align_bytes=64) for h in range(2)]
+        q_codes = [sb.tile([P, NQ], U32, name=f"q_codes{o}", align_bytes=64) for o in range(PASSES)]
+        q_scales = [sb.tile([P, NQ], U8, name=f"q_scales{o}", align_bytes=64) for o in range(PASSES)]
+
+        def part_words(h):
+            nc.vector.tensor_copy(keys[h][:], picked[h][:].bitcast(U16).rearrange("p (n o) -> p o n", o=PASSES))
+
+        for h in range(2):
+            nc.vector.tensor_copy(
+                picked[h][:], word_pool[:].bitcast(U32).indirect(offsets[:, h * HALF // 16 : (h + 1) * HALF // 16])
+            )
+        part_words(0)
         for o in range(PASSES):
-            nc.scalar.copy(out=q_grouped[:, o], in_=q_raw[o][:].rearrange("p j w -> p w j"))
-        nc.vector.quantize_mx(
-            out=q_codes[:].rearrange("p o w -> p (o w)").bitcast(FP8X4),
-            scales=q_scales[:].rearrange("p o w -> p (o w)"),
-            in_=q_grouped[:].rearrange("p o w j -> p (o w j)"),
-        )
+            q_grouped = sb.tile([P, NQ, PACK], BF16, name=f"q_grouped{o}", align_bytes=64)
+            nc.scalar.copy(
+                out=q_grouped[:].rearrange("p (c i) j -> p c j i", i=4),
+                in_=q_raw[o][:].rearrange("p j (c i) -> p c j i", i=4),
+            )
+            nc.vector.quantize_mx(
+                out=q_codes[o][:].bitcast(FP8X4),
+                scales=q_scales[o][:],
+                in_=q_grouped[:].rearrange("p w j -> p (w j)"),
+            )
+        part_words(1)
 
         banks = []
         for h in range(2):
-            picked = sb.tile([P, HALF], U32, name=f"picked{h}", align_bytes=64)
-            nc.vector.tensor_copy(
-                picked[:], word_pool[:].bitcast(U32).indirect(offsets[:, h * HALF // 16 : (h + 1) * HALF // 16])
-            )
-            keys = sb.tile([P, PASSES, HALF], U16, name=f"keys{h}", align_bytes=64)
-            nc.vector.tensor_copy(keys[:], picked[:].bitcast(U16).rearrange("p (n o) -> p o n", o=PASSES))
             bank = psum.tile([P, HALF], F32, name=f"bank{h}")
             for g in range(HALF // GROUP):
                 cols = slice(g * GROUP, (g + 1) * GROUP)
@@ -84,9 +92,9 @@ def tile_attend_nrm_minmax_topk_kernel(tc, qT, k_words, k_scales, offs, out):
                 for o in range(PASSES):
                     nc.tensor.matmul_mx(
                         out=bank[:, cols],
-                        lhsT=q_codes[:, o, :].bitcast(FP8X4),
-                        lhsT_scale=q_scales[:, o, :],
-                        rhs=keys[:, o, cols].bitcast(FP4X4),
+                        lhsT=q_codes[o][:].bitcast(FP8X4),
+                        lhsT_scale=q_scales[o][:],
+                        rhs=keys[h][:, o, cols].bitcast(FP4X4),
                         rhs_scale=planes[:, o, slots],
                         start=(o == 0),
                         stop=(o == PASSES - 1),

@@ -36,25 +36,26 @@ def tile_attend_nrm_minmax_topk_kernel(tc, qT, k_words, k_scales, offs, out):
         word_pool = sb.tile([P, T], I32, name="word_pool", align_bytes=64)
         q_raw = [sb.tile([P, PACK, NQ], F32, name=f"q_raw{o}") for o in range(PASSES)]
 
-        nc.vector.memset(scale_pool[:].bitcast(I32), 0)
+        nc.vector.memset(scale_pool[32:64, :].bitcast(I32), 0)
+        nc.vector.memset(scale_pool[64:P, :].bitcast(I32), 0)
         nc.vector.memset(planes[:].rearrange("p o n -> p (o n)").bitcast(I32), 0)
 
         q_rows = qT[0].rearrange("(o p j) w -> o p j w", o=PASSES, j=PACK)
-        nc.scalar.dma_start(out=word_pool[:], in_=k_words[0].rearrange("p t b -> p (t b)").bitcast(I32))
-        for o in range(PASSES):
-            nc.scalar.dma_start(out=q_raw[o][:], in_=q_rows[o])
         nc.sync.dma_start(offsets[:], offs)
         nc.sync.dma_start(
-            out=scale_pool[0:P:4, :].bitcast(I32),
+            out=scale_pool[0:32, :].bitcast(I32),
             in_=k_scales.rearrange("o f t -> f o t").bitcast(I32),
         )
+        nc.sync.dma_start(out=word_pool[:], in_=k_words[0].rearrange("p t b -> p (t b)").bitcast(I32))
+        for o in range(PASSES):
+            nc.sync.dma_start(out=q_raw[o][:], in_=q_rows[o])
 
         picked_scales = sb.tile([P, N], U8, name="picked_scales", align_bytes=64)
         nc.vector.tensor_copy(picked_scales[:], scale_pool[:].indirect(offsets[:]))
         for quad in range(0, P, 32):
             nc.sync.dma_start(
                 out=planes[quad : quad + 4].rearrange("p o n -> p (o n)").bitcast(I32),
-                in_=picked_scales[quad : quad + 32 : 4, :].bitcast(I32),
+                in_=picked_scales[quad // 4 : quad // 4 + 8, :].bitcast(I32),
             )
 
         picked = [sb.tile([P, HALF], U32, name=f"picked{h}", align_bytes=64) for h in range(2)]

@@ -59,18 +59,17 @@ def tile_attend_nrm_minmax_topk_kernel(tc, qT, k_words, k_scales, offs, out):
             )
 
         picked = [sb.tile([P, HALF], U32, name=f"picked{h}", align_bytes=64) for h in range(2)]
-        keys = [sb.tile([P, PASSES, HALF], U16, name=f"keys{h}", align_bytes=64) for h in range(2)]
+        keys = [sb.tile([P, HALF // GROUP, PASSES, GROUP], U16, name=f"keys{h}", align_bytes=64) for h in range(2)]
         q_codes = [sb.tile([P, NQ], U32, name=f"q_codes{o}", align_bytes=64) for o in range(PASSES)]
         q_scales = [sb.tile([P, NQ], U8, name=f"q_scales{o}", align_bytes=64) for o in range(PASSES)]
 
         def part_words(h):
-            nc.vector.tensor_copy(keys[h][:], picked[h][:].bitcast(U16).rearrange("p (n o) -> p o n", o=PASSES))
+            nc.vector.tensor_copy(keys[h][:], picked[h][:].bitcast(U16).rearrange("p (g n o) -> p g o n", n=GROUP, o=PASSES))
 
         for h in range(2):
             nc.vector.tensor_copy(
                 picked[h][:], word_pool[:].bitcast(U32).indirect(offsets[:, h * HALF // 16 : (h + 1) * HALF // 16])
             )
-        part_words(0)
         for o in range(PASSES):
             q_grouped = sb.tile([P, NQ, PACK], BF16, name=f"q_grouped{o}", align_bytes=64)
             nc.scalar.copy(
@@ -82,7 +81,7 @@ def tile_attend_nrm_minmax_topk_kernel(tc, qT, k_words, k_scales, offs, out):
                 scales=q_scales[o][:],
                 in_=q_grouped[:].rearrange("p w j -> p (w j)"),
             )
-        part_words(1)
+            part_words(o)
 
         banks = []
         for h in range(2):
@@ -95,29 +94,29 @@ def tile_attend_nrm_minmax_topk_kernel(tc, qT, k_words, k_scales, offs, out):
                         out=bank[:, cols],
                         lhsT=q_codes[o][:].bitcast(FP8X4),
                         lhsT_scale=q_scales[o][:],
-                        rhs=keys[h][:, o, cols].bitcast(FP4X4),
+                        rhs=keys[h][:, g, o, :].bitcast(FP4X4),
                         rhs_scale=planes[:, o, slots],
                         start=(o == 0),
                         stop=(o == PASSES - 1),
                     )
             banks.append(bank)
 
-        hi = [sb.tile([P, 1], F32, name=f"hi{h}") for h in range(2)]
-        lo = [sb.tile([P, 1], F32, name=f"lo{h}") for h in range(2)]
-        scores = [sb.tile([P, HALF], F32, name=f"scores{h}") for h in range(2)]
-        spare = [sb.tile([P, HALF], F32, name=f"spare{h}") for h in range(2)]
-        for h in range(2):
-            nc.vector.tensor_scalar(
-                scores[h][:], banks[h][:], 1.0, hi[0][:] if h else None, ALU.mult, ALU.max, accum_out=hi[h][:]
-            )
-            nc.vector.tensor_scalar(
-                spare[h][:], banks[h][:], 1.0, lo[0][:] if h else None, ALU.mult, ALU.min, accum_out=lo[h][:]
-            )
+        first = sb.tile([P, HALF], F32, name="first")
+        second = sb.tile([P, HALF + 1], F32, name="second")
+        lo_first = sb.tile([P, 1], F32, name="lo_first")
+        lo = sb.tile([P, 1], F32, name="lo")
+        nc.vector.tensor_reduce(lo_first[:], banks[0][:], mybir.AxisListType.X, ALU.min)
+        nc.vector.tensor_scalar(
+            first[:], banks[0][:], 1.0, None, ALU.mult, ALU.max, accum_out=second[:, HALF : HALF + 1]
+        )
+        nc.vector.tensor_scalar(second[:, :HALF], banks[1][:], 1.0, lo_first[:], ALU.mult, ALU.min, accum_out=lo[:])
+        above_lo = sb.tile([P, HALF + 1], F32, name="above_lo")
         span = sb.tile([P, 1], F32, name="span")
         inv_span = sb.tile([P, 1], F32, name="inv_span")
-        nc.vector.tensor_tensor(span[:], hi[1][:], lo[1][:], ALU.subtract)
+        nc.vector.tensor_scalar(above_lo[:], second[:], lo[:], None, ALU.subtract, ALU.max, accum_out=span[:])
         nc.vector.reciprocal(inv_span[:], span[:])
-        for h, queue in enumerate((nc.sync, nc.scalar)):
-            result = sb.tile([P, HALF], F32, name=f"result{h}")
-            nc.vector.tensor_scalar(result[:], scores[h][:], lo[1][:], inv_span[:], ALU.subtract, ALU.mult)
-            queue.dma_start(out=out[0, :, h * HALF : (h + 1) * HALF], in_=result[:])
+        results = [sb.tile([P, HALF], F32, name=f"result{h}") for h in range(2)]
+        nc.vector.tensor_scalar(results[0][:], first[:], lo[:], inv_span[:], ALU.subtract, ALU.mult)
+        nc.sync.dma_start(out=out[0, :, :HALF], in_=results[0][:])
+        nc.vector.tensor_scalar(results[1][:], above_lo[:, :HALF], inv_span[:], None, ALU.mult)
+        nc.scalar.dma_start(out=out[0, :, HALF:], in_=results[1][:])

@@ -40,6 +40,11 @@ def tile_attend_nrm_minmax_topk_kernel(tc, qT, k_words, k_scales, offs, out):
         nc.vector.memset(scale_pool[64:P, :].bitcast(I32), 0)
         nc.vector.memset(planes[:].rearrange("p o n -> p (o n)").bitcast(I32), 0)
 
+        warm_in = sb.tile([P, 1], F32, name="warm_in")
+        warm_out = sb.tile([P, 1], BF16, name="warm_out")
+        nc.gpsimd.memset(warm_in[:], 0.0)
+        nc.scalar.copy(out=warm_out[:], in_=warm_in[:])
+
         q_rows = qT[0].rearrange("(o p j) w -> o p j w", o=PASSES, j=PACK)
         nc.sync.dma_start(offsets[:], offs)
         nc.sync.dma_start(
@@ -52,8 +57,8 @@ def tile_attend_nrm_minmax_topk_kernel(tc, qT, k_words, k_scales, offs, out):
 
         picked_scales = sb.tile([P, N], U8, name="picked_scales", align_bytes=64)
         nc.vector.tensor_copy(picked_scales[:], scale_pool[:].indirect(offsets[:]))
-        for quad in range(0, P, 32):
-            nc.sync.dma_start(
+        for quad, queue in zip(range(0, P, 32), (nc.sync, nc.scalar, nc.sync, nc.scalar)):
+            queue.dma_start(
                 out=planes[quad : quad + 4].rearrange("p o n -> p (o n)").bitcast(I32),
                 in_=picked_scales[quad // 4 : quad // 4 + 8, :].bitcast(I32),
             )

@@ -11,6 +11,7 @@ U8 = mybir.dt.uint8
 FP8X4 = mybir.dt.float8_e4m3fn_x4
 FP4X4 = mybir.dt.float4_e2m1fn_x4
 ALU = mybir.AluOpType
+ACT = mybir.ActivationFunctionType
 
 P = 128
 PACK = 4
@@ -41,16 +42,16 @@ def tile_attend_nrm_minmax_topk_kernel(tc, qT, k_words, k_scales, offs, out):
         nc.vector.memset(planes[:].rearrange("p o n -> p (o n)").bitcast(I32), 0)
 
         warm_in = sb.tile([P, 1], F32, name="warm_in")
-        warm_out = sb.tile([P, 1], BF16, name="warm_out")
-        nc.gpsimd.memset(warm_in[:], 0.0)
-        nc.scalar.copy(out=warm_out[:], in_=warm_in[:])
+        warm_out = sb.tile([P, 1], F32, name="warm_out")
+        nc.gpsimd.memset(warm_in[:], 1.0)
+        nc.scalar.activation(warm_out[:], warm_in[:], ACT.Abs_reciprocal_sqrt)
 
         q_rows = qT[0].rearrange("(o p j) w -> o p j w", o=PASSES, j=PACK)
-        nc.sync.dma_start(offsets[:], offs)
         nc.sync.dma_start(
             out=scale_pool[0:32, :].bitcast(I32),
             in_=k_scales.rearrange("o f t -> f o t").bitcast(I32),
         )
+        nc.sync.dma_start(offsets[:], offs)
         nc.sync.dma_start(out=word_pool[:], in_=k_words[0].rearrange("p t b -> p (t b)").bitcast(I32))
         for o in range(PASSES):
             nc.sync.dma_start(out=q_raw[o][:], in_=q_rows[o])
@@ -106,22 +107,22 @@ def tile_attend_nrm_minmax_topk_kernel(tc, qT, k_words, k_scales, offs, out):
                     )
             banks.append(bank)
 
-        first = sb.tile([P, HALF], F32, name="first")
-        second = sb.tile([P, HALF + 1], F32, name="second")
+        scores = [sb.tile([P, HALF], F32, name=f"scores{h}") for h in range(2)]
+        spare = sb.tile([P, HALF], F32, name="spare")
         lo_first = sb.tile([P, 1], F32, name="lo_first")
+        hi_first = sb.tile([P, 1], F32, name="hi_first")
         lo = sb.tile([P, 1], F32, name="lo")
+        hi = sb.tile([P, 1], F32, name="hi")
+        root = sb.tile([P, 1], F32, name="root")
         nc.vector.tensor_reduce(lo_first[:], banks[0][:], mybir.AxisListType.X, ALU.min)
-        nc.vector.tensor_scalar(
-            first[:], banks[0][:], 1.0, None, ALU.mult, ALU.max, accum_out=second[:, HALF : HALF + 1]
-        )
-        nc.vector.tensor_scalar(second[:, :HALF], banks[1][:], 1.0, lo_first[:], ALU.mult, ALU.min, accum_out=lo[:])
-        above_lo = sb.tile([P, HALF + 1], F32, name="above_lo")
-        span = sb.tile([P, 1], F32, name="span")
-        inv_span = sb.tile([P, 1], F32, name="inv_span")
-        nc.vector.tensor_scalar(above_lo[:], second[:], lo[:], None, ALU.subtract, ALU.max, accum_out=span[:])
-        nc.vector.reciprocal(inv_span[:], span[:])
+        nc.vector.tensor_scalar(scores[0][:], banks[0][:], 1.0, None, ALU.mult, ALU.max, accum_out=hi_first[:])
+        nc.vector.tensor_scalar(scores[1][:], banks[1][:], 1.0, lo_first[:], ALU.mult, ALU.min, accum_out=lo[:])
+        nc.vector.tensor_scalar(spare[:], banks[1][:], 1.0, hi_first[:], ALU.mult, ALU.max, accum_out=hi[:])
+        nc.scalar.activation(root[:], lo[:], ACT.Abs_reciprocal_sqrt, bias=hi[:], scale=-1.0)
+        above = [sb.tile([P, HALF], F32, name=f"above{h}") for h in range(2)]
         results = [sb.tile([P, HALF], F32, name=f"result{h}") for h in range(2)]
-        nc.vector.tensor_scalar(results[0][:], first[:], lo[:], inv_span[:], ALU.subtract, ALU.mult)
-        nc.sync.dma_start(out=out[0, :, :HALF], in_=results[0][:])
-        nc.vector.tensor_scalar(results[1][:], above_lo[:, :HALF], inv_span[:], None, ALU.mult)
-        nc.scalar.dma_start(out=out[0, :, HALF:], in_=results[1][:])
+        for h in range(2):
+            nc.vector.tensor_scalar(above[h][:], scores[h][:], lo[:], None, ALU.subtract)
+        for h, queue in enumerate((nc.sync, nc.scalar)):
+            nc.vector.tensor_scalar(results[h][:], above[h][:], root[:], root[:], ALU.mult, ALU.mult)
+            queue.dma_start(out=out[0, :, h * HALF : (h + 1) * HALF], in_=results[h][:])

@@ -35,7 +35,7 @@ def tile_attend_nrm_minmax_topk_kernel(tc, qT, k_words, k_scales, offs, out):
         scale_pool = sb.tile([P, T], U8, name="scale_pool", align_bytes=64)
         planes = sb.tile([P, PASSES, N], U8, name="planes", align_bytes=64)
         word_pool = sb.tile([P, T], I32, name="word_pool", align_bytes=64)
-        q_raw = [sb.tile([P, PACK, NQ], F32, name=f"q_raw{o}") for o in range(PASSES)]
+        q_raw = [sb.tile([P, PACK, NQ], F32, name=f"q_raw{o}", tag=f"raw{o}", align_bytes=64) for o in range(PASSES)]
 
         nc.vector.memset(scale_pool[32:64, :].bitcast(I32), 0)
         nc.vector.memset(scale_pool[64:P, :].bitcast(I32), 0)
@@ -43,7 +43,7 @@ def tile_attend_nrm_minmax_topk_kernel(tc, qT, k_words, k_scales, offs, out):
 
         warm_in = sb.tile([P, 1], F32, name="warm_in")
         warm_out = sb.tile([P, 1], F32, name="warm_out")
-        nc.gpsimd.memset(warm_in[:], 1.0)
+        nc.vector.memset(warm_in[:], 1.0)
         nc.scalar.activation(warm_out[:], warm_in[:], ACT.Abs_reciprocal_sqrt)
 
         q_rows = qT[0].rearrange("(o p j) w -> o p j w", o=PASSES, j=PACK)
@@ -65,64 +65,80 @@ def tile_attend_nrm_minmax_topk_kernel(tc, qT, k_words, k_scales, offs, out):
             )
 
         picked = [sb.tile([P, HALF], U32, name=f"picked{h}", align_bytes=64) for h in range(2)]
-        keys = [sb.tile([P, HALF // GROUP, PASSES, GROUP], U16, name=f"keys{h}", align_bytes=64) for h in range(2)]
         q_codes = [sb.tile([P, NQ], U32, name=f"q_codes{o}", align_bytes=64) for o in range(PASSES)]
         q_scales = [sb.tile([P, NQ], U8, name=f"q_scales{o}", align_bytes=64) for o in range(PASSES)]
+        keys = {}
 
-        def part_words(h):
-            nc.vector.tensor_copy(keys[h][:], picked[h][:].bitcast(U16).rearrange("p (g n o) -> p g o n", n=GROUP, o=PASSES))
+        def part_words(first_group, groups, tile):
+            h, first = divmod(first_group * GROUP, HALF)
+            for g in range(groups):
+                for o in range(PASSES):
+                    keys[first_group + g, o] = tile[:, o, g * GROUP : (g + 1) * GROUP]
+            nc.vector.tensor_copy(
+                tile.rearrange("p o (u n) -> p u o n", u=2),
+                picked[h][:, first : first + groups * GROUP].bitcast(U16).rearrange("p (u n o) -> p u o n", u=2, o=PASSES),
+            )
+
+        def cast(o, rows, name):
+            width = rows.stop - rows.start
+            q_grouped = sb.tile([P, width, PACK], BF16, name=name, tag=name, align_bytes=64)
+            nc.scalar.copy(
+                out=q_grouped[:].rearrange("p (c i) j -> p c j i", i=4),
+                in_=q_raw[o][:, :, rows].rearrange("p j (c i) -> p c j i", i=4),
+            )
+            return q_grouped
+
+        def quantise(o, rows, q_grouped):
+            nc.vector.quantize_mx(
+                out=q_codes[o][:, rows].bitcast(FP8X4),
+                scales=q_scales[o][:, rows],
+                in_=q_grouped[:].rearrange("p w j -> p (w j)"),
+            )
 
         for h in range(2):
             nc.vector.tensor_copy(
                 picked[h][:], word_pool[:].bitcast(U32).indirect(offsets[:, h * HALF // 16 : (h + 1) * HALF // 16])
             )
-        for o in range(PASSES):
-            q_grouped = sb.tile([P, NQ, PACK], BF16, name=f"q_grouped{o}", align_bytes=64)
-            nc.scalar.copy(
-                out=q_grouped[:].rearrange("p (c i) j -> p c j i", i=4),
-                in_=q_raw[o][:].rearrange("p j (c i) -> p c j i", i=4),
-            )
-            nc.vector.quantize_mx(
-                out=q_codes[o][:].bitcast(FP8X4),
-                scales=q_scales[o][:],
-                in_=q_grouped[:].rearrange("p w j -> p (w j)"),
-            )
-            part_words(o)
+        keys_first = sb.tile([P, PASSES, HALF], U16, name="keys_first", align_bytes=64)
+        part_words(0, 2, keys_first[:])
+        pieces = ((0, slice(0, NQ)), (1, slice(0, NQ // 2)), (1, slice(NQ // 2, NQ)))
+        grouped = [cast(o, rows, f"grouped{i}") for i, (o, rows) in enumerate(pieces)]
+        for (o, rows), q_grouped in zip(pieces, grouped):
+            quantise(o, rows, q_grouped)
+        keys_last = sb.tile([P, 2, PASSES, GROUP], U16, name="keys_last", tag="grouped2", align_bytes=64)
+        for g in range(2):
+            part_words(2 + g, 1, keys_last[:, g])
 
-        banks = []
-        for h in range(2):
-            bank = psum.tile([P, HALF], F32, name=f"bank{h}")
-            for g in range(HALF // GROUP):
-                cols = slice(g * GROUP, (g + 1) * GROUP)
-                slots = slice(h * HALF + g * GROUP, h * HALF + (g + 1) * GROUP)
-                for o in range(PASSES):
-                    nc.tensor.matmul_mx(
-                        out=bank[:, cols],
-                        lhsT=q_codes[o][:].bitcast(FP8X4),
-                        lhsT_scale=q_scales[o][:],
-                        rhs=keys[h][:, g, o, :].bitcast(FP4X4),
-                        rhs_scale=planes[:, o, slots],
-                        start=(o == 0),
-                        stop=(o == PASSES - 1),
-                    )
-            banks.append(bank)
+        banks = [psum.tile([P, HALF], F32, name=f"bank{h}") for h in range(2)]
+        for g in range(N // GROUP):
+            h, first = divmod(g * GROUP, HALF)
+            for o in range(PASSES):
+                nc.tensor.matmul_mx(
+                    out=banks[h][:, first : first + GROUP],
+                    lhsT=q_codes[o][:].bitcast(FP8X4),
+                    lhsT_scale=q_scales[o][:],
+                    rhs=keys[g, o].bitcast(FP4X4),
+                    rhs_scale=planes[:, o, g * GROUP : (g + 1) * GROUP],
+                    start=(o == 0),
+                    stop=(o == PASSES - 1),
+                )
 
-        scores = [sb.tile([P, HALF], F32, name=f"scores{h}") for h in range(2)]
+        flipped = sb.tile([P, HALF], F32, name="flipped")
         spare = sb.tile([P, HALF], F32, name="spare")
-        lo_first = sb.tile([P, 1], F32, name="lo_first")
+        neg_lo_first = sb.tile([P, 1], F32, name="neg_lo_first")
         hi_first = sb.tile([P, 1], F32, name="hi_first")
-        lo = sb.tile([P, 1], F32, name="lo")
+        neg_lo = sb.tile([P, 1], F32, name="neg_lo")
         hi = sb.tile([P, 1], F32, name="hi")
         root = sb.tile([P, 1], F32, name="root")
-        nc.vector.tensor_reduce(lo_first[:], banks[0][:], mybir.AxisListType.X, ALU.min)
-        nc.vector.tensor_scalar(scores[0][:], banks[0][:], 1.0, None, ALU.mult, ALU.max, accum_out=hi_first[:])
-        nc.vector.tensor_scalar(scores[1][:], banks[1][:], 1.0, lo_first[:], ALU.mult, ALU.min, accum_out=lo[:])
-        nc.vector.tensor_scalar(spare[:], banks[1][:], 1.0, hi_first[:], ALU.mult, ALU.max, accum_out=hi[:])
-        nc.scalar.activation(root[:], lo[:], ACT.Abs_reciprocal_sqrt, bias=hi[:], scale=-1.0)
         above = [sb.tile([P, HALF], F32, name=f"above{h}") for h in range(2)]
         results = [sb.tile([P, HALF], F32, name=f"result{h}") for h in range(2)]
-        for h in range(2):
-            nc.vector.tensor_scalar(above[h][:], scores[h][:], lo[:], None, ALU.subtract)
-        for h, queue in enumerate((nc.sync, nc.scalar)):
+        nc.vector.tensor_reduce(neg_lo_first[:], banks[0][:], mybir.AxisListType.X, ALU.min, negate=True)
+        nc.vector.tensor_reduce(hi_first[:], banks[0][:], mybir.AxisListType.X, ALU.max)
+        nc.vector.tensor_scalar(flipped[:], banks[1][:], -1.0, neg_lo_first[:], ALU.mult, ALU.max, accum_out=neg_lo[:])
+        nc.vector.tensor_scalar(spare[:], banks[1][:], 1.0, hi_first[:], ALU.mult, ALU.max, accum_out=hi[:])
+        nc.scalar.activation(above[0][:], banks[0][:], ACT.Identity, bias=neg_lo[:], scale=1.0)
+        nc.scalar.activation(root[:], neg_lo[:], ACT.Abs_reciprocal_sqrt, bias=hi[:], scale=1.0)
+        nc.vector.tensor_scalar(above[1][:], flipped[:], -1.0, neg_lo[:], ALU.mult, ALU.add)
+        for h, queue in zip((1, 0), (nc.sync, nc.scalar)):
             nc.vector.tensor_scalar(results[h][:], above[h][:], root[:], root[:], ALU.mult, ALU.mult)
             queue.dma_start(out=out[0, :, h * HALF : (h + 1) * HALF], in_=results[h][:])

@@ -101,11 +101,11 @@ def tile_attend_nrm_minmax_topk_kernel(tc, qT, k_words, k_scales, offs, out):
             )
         keys_first = sb.tile([P, PASSES, HALF], U16, name="keys_first", align_bytes=64)
         part_words(0, 2, keys_first[:])
-        pieces = ((0, slice(0, NQ)), (1, slice(0, NQ // 2)), (1, slice(NQ // 2, NQ)))
+        pieces = [(o, slice(r, r + NQ // 2)) for o in range(PASSES) for r in (0, NQ // 2)]
         grouped = [cast(o, rows, f"grouped{i}") for i, (o, rows) in enumerate(pieces)]
         for (o, rows), q_grouped in zip(pieces, grouped):
             quantise(o, rows, q_grouped)
-        keys_last = sb.tile([P, 2, PASSES, GROUP], U16, name="keys_last", tag="grouped2", align_bytes=64)
+        keys_last = sb.tile([P, 2, PASSES, GROUP], U16, name="keys_last", tag="grouped3", align_bytes=64)
         for g in range(2):
             part_words(2 + g, 1, keys_last[:, g])
 
@@ -130,15 +130,15 @@ def tile_attend_nrm_minmax_topk_kernel(tc, qT, k_words, k_scales, offs, out):
         neg_lo = sb.tile([P, 1], F32, name="neg_lo")
         hi = sb.tile([P, 1], F32, name="hi")
         root = sb.tile([P, 1], F32, name="root")
-        above = [sb.tile([P, HALF], F32, name=f"above{h}") for h in range(2)]
-        results = [sb.tile([P, HALF], F32, name=f"result{h}") for h in range(2)]
+        above = sb.tile([P, N], F32, name="above")
+        result = sb.tile([P, N], F32, name="result")
         nc.vector.tensor_reduce(neg_lo_first[:], banks[0][:], mybir.AxisListType.X, ALU.min, negate=True)
         nc.vector.tensor_reduce(hi_first[:], banks[0][:], mybir.AxisListType.X, ALU.max)
         nc.vector.tensor_scalar(flipped[:], banks[1][:], -1.0, neg_lo_first[:], ALU.mult, ALU.max, accum_out=neg_lo[:])
         nc.vector.tensor_scalar(spare[:], banks[1][:], 1.0, hi_first[:], ALU.mult, ALU.max, accum_out=hi[:])
-        nc.scalar.activation(above[0][:], banks[0][:], ACT.Identity, bias=neg_lo[:], scale=1.0)
+        nc.scalar.activation(above[:, 0:HALF], banks[0][:], ACT.Identity, bias=neg_lo[:], scale=1.0)
         nc.scalar.activation(root[:], neg_lo[:], ACT.Abs_reciprocal_sqrt, bias=hi[:], scale=1.0)
-        nc.vector.tensor_scalar(above[1][:], flipped[:], -1.0, neg_lo[:], ALU.mult, ALU.add)
-        for h, queue in zip((1, 0), (nc.sync, nc.scalar)):
-            nc.vector.tensor_scalar(results[h][:], above[h][:], root[:], root[:], ALU.mult, ALU.mult)
-            queue.dma_start(out=out[0, :, h * HALF : (h + 1) * HALF], in_=results[h][:])
+        nc.vector.tensor_scalar(above[:, HALF:N], flipped[:], -1.0, neg_lo[:], ALU.mult, ALU.add)
+        for cols, queue in ((slice(0, GROUP), nc.sync), (slice(GROUP, N), nc.scalar)):
+            nc.vector.tensor_scalar(result[:, cols], above[:, cols], root[:], root[:], ALU.mult, ALU.mult)
+            queue.dma_start(out=out[0, :, cols], in_=result[:, cols])

@@ -14,6 +14,7 @@ ALU = mybir.AluOpType
 ACT = mybir.ActivationFunctionType
 
 P = 128
+QUADRANT = 32
 PACK = 4
 PASSES = 2
 T = 2048
@@ -21,6 +22,9 @@ N = 512
 NQ = 128
 HALF = N // 2
 GROUP = 128
+PIECE = NQ // 2
+STRIPE = 16
+FIRST_STORE = 192
 
 FLOPS = 2 * NQ * N * PASSES * P * PACK
 
@@ -31,24 +35,24 @@ def tile_attend_nrm_minmax_topk_kernel(tc, qT, k_words, k_scales, offs, out):
         sb = ctx.enter_context(tc.tile_pool(name="sb", bufs=1))
         psum = ctx.enter_context(tc.psum_pool(name="psum", bufs=1))
 
-        offsets = sb.tile([P, N // 16], U16, name="offsets")
+        offsets = sb.tile([P, N // STRIPE], U16, name="offsets")
         scale_pool = sb.tile([P, T], U8, name="scale_pool", align_bytes=64)
         planes = sb.tile([P, PASSES, N], U8, name="planes", align_bytes=64)
         word_pool = sb.tile([P, T], I32, name="word_pool", align_bytes=64)
-        q_raw = [sb.tile([P, PACK, NQ], F32, name=f"q_raw{o}", tag=f"raw{o}", align_bytes=64) for o in range(PASSES)]
+        q_raw = [sb.tile([P, PACK, NQ], F32, name=f"q_raw{o}", align_bytes=64) for o in range(PASSES)]
 
-        nc.vector.memset(scale_pool[32:64, :].bitcast(I32), 0)
-        nc.vector.memset(scale_pool[64:P, :].bitcast(I32), 0)
+        nc.vector.memset(scale_pool[QUADRANT : 2 * QUADRANT, :].bitcast(I32), 0)
+        nc.vector.memset(scale_pool[2 * QUADRANT : P, :].bitcast(I32), 0)
         nc.vector.memset(planes[:].rearrange("p o n -> p (o n)").bitcast(I32), 0)
 
-        warm_in = sb.tile([P, 1], F32, name="warm_in")
-        warm_out = sb.tile([P, 1], F32, name="warm_out")
-        nc.vector.memset(warm_in[:], 1.0)
-        nc.scalar.activation(warm_out[:], warm_in[:], ACT.Abs_reciprocal_sqrt)
+        table_in = sb.tile([P, 1], F32, name="table_in")
+        table_out = sb.tile([P, 1], F32, name="table_out")
+        nc.vector.memset(table_in[:], 1.0)
+        nc.scalar.activation(table_out[:], table_in[:], ACT.Abs_reciprocal_sqrt)
 
-        q_rows = qT[0].rearrange("(o p j) w -> o p j w", o=PASSES, j=PACK)
+        q_rows = qT[0].rearrange("(o p r) w -> o p r w", o=PASSES, r=PACK)
         nc.sync.dma_start(
-            out=scale_pool[0:32, :].bitcast(I32),
+            out=scale_pool[0:QUADRANT, :].bitcast(I32),
             in_=k_scales.rearrange("o f t -> f o t").bitcast(I32),
         )
         nc.sync.dma_start(offsets[:], offs)
@@ -58,10 +62,10 @@ def tile_attend_nrm_minmax_topk_kernel(tc, qT, k_words, k_scales, offs, out):
 
         picked_scales = sb.tile([P, N], U8, name="picked_scales", align_bytes=64)
         nc.vector.tensor_copy(picked_scales[:], scale_pool[:].indirect(offsets[:]))
-        for quad, queue in zip(range(0, P, 32), (nc.sync, nc.scalar, nc.sync, nc.scalar)):
+        for j, queue in enumerate((nc.sync, nc.scalar, nc.sync, nc.scalar)):
             queue.dma_start(
-                out=planes[quad : quad + 4].rearrange("p o n -> p (o n)").bitcast(I32),
-                in_=picked_scales[quad // 4 : quad // 4 + 8, :].bitcast(I32),
+                out=planes[QUADRANT * j : QUADRANT * j + 4].rearrange("p o n -> p (o n)").bitcast(I32),
+                in_=picked_scales[8 * j : 8 * j + 8, :].bitcast(I32),
             )
 
         picked = [sb.tile([P, HALF], U32, name=f"picked{h}", align_bytes=64) for h in range(2)]
@@ -80,34 +84,33 @@ def tile_attend_nrm_minmax_topk_kernel(tc, qT, k_words, k_scales, offs, out):
             )
 
         def cast(o, rows, name):
-            width = rows.stop - rows.start
-            q_grouped = sb.tile([P, width, PACK], BF16, name=name, tag=name, align_bytes=64)
+            q_grouped = sb.tile([P, PIECE, PACK], BF16, name=name, tag=name, align_bytes=64)
             nc.scalar.copy(
-                out=q_grouped[:].rearrange("p (c i) j -> p c j i", i=4),
-                in_=q_raw[o][:, :, rows].rearrange("p j (c i) -> p c j i", i=4),
+                out=q_grouped[:].rearrange("p (c i) r -> p c r i", i=4),
+                in_=q_raw[o][:, :, rows].rearrange("p r (c i) -> p c r i", i=4),
             )
             return q_grouped
 
-        def quantise(o, rows, q_grouped):
+        for h in range(2):
+            nc.vector.tensor_copy(
+                picked[h][:],
+                word_pool[:].bitcast(U32).indirect(offsets[:, h * HALF // STRIPE : (h + 1) * HALF // STRIPE]),
+            )
+        keys_first = sb.tile([P, PASSES, HALF], U16, name="keys_first", align_bytes=64)
+        part_words(0, HALF // GROUP, keys_first[:])
+
+        pieces = [(o, slice(r, r + PIECE)) for o in range(PASSES) for r in range(0, NQ, PIECE)]
+        names = [f"grouped{i}" for i in range(len(pieces))]
+        grouped = [cast(o, rows, name) for (o, rows), name in zip(pieces, names)]
+        for (o, rows), q_grouped in zip(pieces, grouped):
             nc.vector.quantize_mx(
                 out=q_codes[o][:, rows].bitcast(FP8X4),
                 scales=q_scales[o][:, rows],
-                in_=q_grouped[:].rearrange("p w j -> p (w j)"),
+                in_=q_grouped[:].rearrange("p w r -> p (w r)"),
             )
-
-        for h in range(2):
-            nc.vector.tensor_copy(
-                picked[h][:], word_pool[:].bitcast(U32).indirect(offsets[:, h * HALF // 16 : (h + 1) * HALF // 16])
-            )
-        keys_first = sb.tile([P, PASSES, HALF], U16, name="keys_first", align_bytes=64)
-        part_words(0, 2, keys_first[:])
-        pieces = [(o, slice(r, r + NQ // 2)) for o in range(PASSES) for r in (0, NQ // 2)]
-        grouped = [cast(o, rows, f"grouped{i}") for i, (o, rows) in enumerate(pieces)]
-        for (o, rows), q_grouped in zip(pieces, grouped):
-            quantise(o, rows, q_grouped)
-        keys_last = sb.tile([P, 2, PASSES, GROUP], U16, name="keys_last", tag="grouped3", align_bytes=64)
-        for g in range(2):
-            part_words(2 + g, 1, keys_last[:, g])
+        keys_last = sb.tile([P, HALF // GROUP, PASSES, GROUP], U16, name="keys_last", tag=names[-1], align_bytes=64)
+        for g in range(HALF // GROUP):
+            part_words(HALF // GROUP + g, 1, keys_last[:, g])
 
         banks = [psum.tile([P, HALF], F32, name=f"bank{h}") for h in range(2)]
         for g in range(N // GROUP):
@@ -124,7 +127,7 @@ def tile_attend_nrm_minmax_topk_kernel(tc, qT, k_words, k_scales, offs, out):
                 )
 
         flipped = sb.tile([P, HALF], F32, name="flipped")
-        spare = sb.tile([P, HALF], F32, name="spare")
+        unread = sb.tile([P, HALF], F32, name="unread")
         neg_lo_first = sb.tile([P, 1], F32, name="neg_lo_first")
         hi_first = sb.tile([P, 1], F32, name="hi_first")
         neg_lo = sb.tile([P, 1], F32, name="neg_lo")
@@ -135,10 +138,13 @@ def tile_attend_nrm_minmax_topk_kernel(tc, qT, k_words, k_scales, offs, out):
         nc.vector.tensor_reduce(neg_lo_first[:], banks[0][:], mybir.AxisListType.X, ALU.min, negate=True)
         nc.vector.tensor_reduce(hi_first[:], banks[0][:], mybir.AxisListType.X, ALU.max)
         nc.vector.tensor_scalar(flipped[:], banks[1][:], -1.0, neg_lo_first[:], ALU.mult, ALU.max, accum_out=neg_lo[:])
-        nc.vector.tensor_scalar(spare[:], banks[1][:], 1.0, hi_first[:], ALU.mult, ALU.max, accum_out=hi[:])
-        nc.scalar.activation(above[:, 0:HALF], banks[0][:], ACT.Identity, bias=neg_lo[:], scale=1.0)
+        nc.vector.tensor_scalar(unread[:], banks[1][:], 1.0, hi_first[:], ALU.mult, ALU.max, accum_out=hi[:])
+
+        for cols in (slice(0, FIRST_STORE), slice(FIRST_STORE, HALF)):
+            nc.scalar.activation(above[:, cols], banks[0][:, cols], ACT.Identity, bias=neg_lo[:], scale=1.0)
         nc.scalar.activation(root[:], neg_lo[:], ACT.Abs_reciprocal_sqrt, bias=hi[:], scale=1.0)
         nc.vector.tensor_scalar(above[:, HALF:N], flipped[:], -1.0, neg_lo[:], ALU.mult, ALU.add)
-        for cols, queue in ((slice(0, GROUP), nc.sync), (slice(GROUP, N), nc.scalar)):
+
+        for cols, queue in ((slice(0, FIRST_STORE), nc.sync), (slice(FIRST_STORE, N), nc.scalar)):
             nc.vector.tensor_scalar(result[:, cols], above[:, cols], root[:], root[:], ALU.mult, ALU.mult)
             queue.dma_start(out=out[0, :, cols], in_=result[:, cols])

@@ -73,14 +73,12 @@ def tile_attend_nrm_minmax_topk_kernel(tc, qT, k_words, k_scales, offs, out):
         q_scales = [sb.tile([P, NQ], U8, name=f"q_scales{o}", align_bytes=64) for o in range(PASSES)]
         keys = {}
 
-        def part_words(first_group, groups, tile):
-            h, first = divmod(first_group * GROUP, HALF)
-            for g in range(groups):
-                for o in range(PASSES):
-                    keys[first_group + g, o] = tile[:, o, g * GROUP : (g + 1) * GROUP]
+        def part_words(h, passes, tile):
+            for i, o in enumerate(range(passes.start, passes.stop)):
+                keys[h, o] = tile[:, i]
             nc.vector.tensor_copy(
                 tile.rearrange("p o (u n) -> p u o n", u=2),
-                picked[h][:, first : first + groups * GROUP].bitcast(U16).rearrange("p (u n o) -> p u o n", u=2, o=PASSES),
+                picked[h][:].bitcast(U16).rearrange("p (u n o) -> p u o n", u=2, o=PASSES)[:, :, passes, :],
             )
 
         def cast(o, rows, name):
@@ -97,33 +95,39 @@ def tile_attend_nrm_minmax_topk_kernel(tc, qT, k_words, k_scales, offs, out):
                 word_pool[:].bitcast(U32).indirect(offsets[:, h * HALF // STRIPE : (h + 1) * HALF // STRIPE]),
             )
         keys_first = sb.tile([P, PASSES, HALF], U16, name="keys_first", align_bytes=64)
-        part_words(0, HALF // GROUP, keys_first[:])
+        part_words(0, slice(0, PASSES), keys_first[:])
 
         pieces = [(o, slice(r, r + PIECE)) for o in range(PASSES) for r in range(0, NQ, PIECE)]
         names = [f"grouped{i}" for i in range(len(pieces))]
         grouped = [cast(o, rows, name) for (o, rows), name in zip(pieces, names)]
-        for (o, rows), q_grouped in zip(pieces, grouped):
+
+        def quantise(i):
+            o, rows = pieces[i]
             nc.vector.quantize_mx(
                 out=q_codes[o][:, rows].bitcast(FP8X4),
                 scales=q_scales[o][:, rows],
-                in_=q_grouped[:].rearrange("p w r -> p (w r)"),
+                in_=grouped[i][:].rearrange("p w r -> p (w r)"),
             )
-        keys_last = sb.tile([P, HALF // GROUP, PASSES, GROUP], U16, name="keys_last", tag=names[-1], align_bytes=64)
-        for g in range(HALF // GROUP):
-            part_words(HALF // GROUP + g, 1, keys_last[:, g])
+
+        for i in range(len(pieces)):
+            quantise(i)
+        keys_last = sb.tile([P, PASSES, HALF], U16, name="keys_last", tag=names[-1], align_bytes=64)
+        for o in range(PASSES):
+            part_words(1, slice(o, o + 1), keys_last[:, o : o + 1])
 
         banks = [psum.tile([P, HALF], F32, name=f"bank{h}") for h in range(2)]
-        for g in range(N // GROUP):
-            h, first = divmod(g * GROUP, HALF)
-            for o in range(PASSES):
+        for h in range(2):
+            steps = [(o, first) for o in range(PASSES) for first in range(0, HALF, GROUP)]
+            for i, (o, first) in enumerate(steps):
+                g = (h * HALF + first) // GROUP
                 nc.tensor.matmul_mx(
                     out=banks[h][:, first : first + GROUP],
                     lhsT=q_codes[o][:].bitcast(FP8X4),
                     lhsT_scale=q_scales[o][:],
-                    rhs=keys[g, o].bitcast(FP4X4),
+                    rhs=keys[h, o][:, first : first + GROUP].bitcast(FP4X4),
                     rhs_scale=planes[:, o, g * GROUP : (g + 1) * GROUP],
-                    start=(o == 0),
-                    stop=(o == PASSES - 1),
+                    start=(i == 0),
+                    stop=(i == len(steps) - 1),
                 )
 
         flipped = sb.tile([P, HALF], F32, name="flipped")

@@ -24,7 +24,6 @@ HALF = N // 2
 GROUP = 128
 PIECE = NQ // 2
 STRIPE = 16
-FIRST_STORE = 192
 
 FLOPS = 2 * NQ * N * PASSES * P * PACK
 
@@ -144,11 +143,9 @@ def tile_attend_nrm_minmax_topk_kernel(tc, qT, k_words, k_scales, offs, out):
         nc.vector.tensor_scalar(flipped[:], banks[1][:], -1.0, neg_lo_first[:], ALU.mult, ALU.max, accum_out=neg_lo[:])
         nc.vector.tensor_scalar(unread[:], banks[1][:], 1.0, hi_first[:], ALU.mult, ALU.max, accum_out=hi[:])
 
-        for cols in (slice(0, FIRST_STORE), slice(FIRST_STORE, HALF)):
-            nc.scalar.activation(above[:, cols], banks[0][:, cols], ACT.Identity, bias=neg_lo[:], scale=1.0)
+        nc.scalar.activation(above[:, 0:HALF], banks[0][:], ACT.Identity, bias=neg_lo[:], scale=1.0)
         nc.scalar.activation(root[:], neg_lo[:], ACT.Abs_reciprocal_sqrt, bias=hi[:], scale=1.0)
         nc.vector.tensor_scalar(above[:, HALF:N], flipped[:], -1.0, neg_lo[:], ALU.mult, ALU.add)
 
-        for cols, queue in ((slice(0, FIRST_STORE), nc.sync), (slice(FIRST_STORE, N), nc.scalar)):
-            nc.vector.tensor_scalar(result[:, cols], above[:, cols], root[:], root[:], ALU.mult, ALU.mult)
-            queue.dma_start(out=out[0, :, cols], in_=result[:, cols])
+        nc.vector.tensor_scalar(result[:], above[:], root[:], root[:], ALU.mult, ALU.mult)
+        nc.sync.dma_start(out=out[0], in_=result[:])

@@ -80,11 +80,11 @@ def tile_attend_nrm_minmax_topk_kernel(tc, qT, k_words, k_scales, offs, out):
                 picked[h][:].bitcast(U16).rearrange("p (u n o) -> p u o n", u=2, o=PASSES)[:, :, passes, :],
             )
 
-        def cast(o, rows, name):
+        def cast(copy, o, rows, name):
             q_grouped = sb.tile([P, PIECE, PACK], BF16, name=name, tag=name, align_bytes=64)
-            nc.scalar.copy(
-                out=q_grouped[:].rearrange("p (c i) r -> p c r i", i=4),
-                in_=q_raw[o][:, :, rows].rearrange("p r (c i) -> p c r i", i=4),
+            copy(
+                q_grouped[:].rearrange("p (c i) r -> p c r i", i=4),
+                q_raw[o][:, :, rows].rearrange("p r (c i) -> p c r i", i=4),
             )
             return q_grouped
 
@@ -98,7 +98,8 @@ def tile_attend_nrm_minmax_topk_kernel(tc, qT, k_words, k_scales, offs, out):
 
         pieces = [(o, slice(r, r + PIECE)) for o in range(PASSES) for r in range(0, NQ, PIECE)]
         names = [f"grouped{i}" for i in range(len(pieces))]
-        grouped = [cast(o, rows, name) for (o, rows), name in zip(pieces, names)]
+        copies = (nc.scalar.copy, nc.scalar.copy, nc.scalar.copy, nc.vector.tensor_copy)
+        grouped = [cast(copy, o, rows, name) for copy, (o, rows), name in zip(copies, pieces, names)]
 
         def quantise(i):
             o, rows = pieces[i]

@@ -35,14 +35,15 @@ def tile_attend_nrm_minmax_topk_kernel(tc, qT, k_words, k_scales, offs, out):
         psum = ctx.enter_context(tc.psum_pool(name="psum", bufs=1))
 
         offsets = sb.tile([P, N // STRIPE], U16, name="offsets")
-        scale_pool = sb.tile([P, T], U8, name="scale_pool", align_bytes=64)
-        planes = sb.tile([P, PASSES, N], U8, name="planes", align_bytes=64)
+        scale_pool = sb.tile([P, T], U8, name="scale_pool", tag="scale_pool", align_bytes=64)
+        planes = [sb.tile([P, PASSES, HALF], U8, name=f"planes{h}", align_bytes=64) for h in range(2)]
         word_pool = sb.tile([P, T], I32, name="word_pool", align_bytes=64)
-        q_raw = [sb.tile([P, PACK, NQ], F32, name=f"q_raw{o}", align_bytes=64) for o in range(PASSES)]
+        q_raw = [sb.tile([P, PACK, NQ], F32, name="q_raw0", align_bytes=64)]
 
         nc.vector.memset(scale_pool[QUADRANT : 2 * QUADRANT, :].bitcast(I32), 0)
         nc.vector.memset(scale_pool[2 * QUADRANT : P, :].bitcast(I32), 0)
-        nc.vector.memset(planes[:].rearrange("p o n -> p (o n)").bitcast(I32), 0)
+        for h in range(2):
+            nc.vector.memset(planes[h][:].rearrange("p o n -> p (o n)").bitcast(I32), 0)
 
         table_in = sb.tile([P, 1], F32, name="table_in")
         table_out = sb.tile([P, 1], F32, name="table_out")
@@ -56,16 +57,25 @@ def tile_attend_nrm_minmax_topk_kernel(tc, qT, k_words, k_scales, offs, out):
         )
         nc.sync.dma_start(offsets[:], offs)
         nc.sync.dma_start(out=word_pool[:], in_=k_words[0].rearrange("p t b -> p (t b)").bitcast(I32))
-        for o in range(PASSES):
-            nc.sync.dma_start(out=q_raw[o][:], in_=q_rows[o])
+        nc.sync.dma_start(out=q_raw[0][:], in_=q_rows[0])
 
-        picked_scales = sb.tile([P, N], U8, name="picked_scales", align_bytes=64)
-        nc.vector.tensor_copy(picked_scales[:], scale_pool[:].indirect(offsets[:]))
-        for j, queue in enumerate((nc.sync, nc.scalar, nc.sync, nc.scalar)):
-            queue.dma_start(
-                out=planes[QUADRANT * j : QUADRANT * j + 4].rearrange("p o n -> p (o n)").bitcast(I32),
-                in_=picked_scales[8 * j : 8 * j + 8, :].bitcast(I32),
-            )
+        def list_half(h):
+            return offsets[:, h * HALF // STRIPE : (h + 1) * HALF // STRIPE]
+
+        def move_scales(h, queues):
+            for j, queue in enumerate(queues):
+                queue.dma_start(
+                    out=planes[h][QUADRANT * j : QUADRANT * j + 4].rearrange("p o n -> p (o n)").bitcast(I32),
+                    in_=picked_scales[h][8 * j : 8 * j + 8, :].bitcast(I32),
+                )
+
+        picked_scales = [sb.tile([P, HALF], U8, name=f"picked_scales{h}", align_bytes=64) for h in range(2)]
+        for h in range(2):
+            nc.vector.tensor_copy(picked_scales[h][:], scale_pool[:].indirect(list_half(h)))
+        move_scales(0, (nc.scalar, nc.sync, nc.scalar, nc.sync))
+        q_raw.append(sb.tile([P, PACK, NQ], F32, name="q_raw1", tag="scale_pool", align_bytes=64))
+        nc.sync.dma_start(out=q_raw[1][:], in_=q_rows[1])
+        move_scales(1, (nc.scalar, nc.sync, nc.sync, nc.sync))
 
         picked = [sb.tile([P, HALF], U32, name=f"picked{h}", align_bytes=64) for h in range(2)]
         q_codes = [sb.tile([P, NQ], U32, name=f"q_codes{o}", align_bytes=64) for o in range(PASSES)]
@@ -89,10 +99,7 @@ def tile_attend_nrm_minmax_topk_kernel(tc, qT, k_words, k_scales, offs, out):
             return q_grouped
 
         for h in range(2):
-            nc.vector.tensor_copy(
-                picked[h][:],
-                word_pool[:].bitcast(U32).indirect(offsets[:, h * HALF // STRIPE : (h + 1) * HALF // STRIPE]),
-            )
+            nc.vector.tensor_copy(picked[h][:], word_pool[:].bitcast(U32).indirect(list_half(h)))
         keys_first = sb.tile([P, PASSES, HALF], U16, name="keys_first", align_bytes=64)
         part_words(0, slice(0, PASSES), keys_first[:])
 
@@ -119,13 +126,12 @@ def tile_attend_nrm_minmax_topk_kernel(tc, qT, k_words, k_scales, offs, out):
         for h in range(2):
             steps = [(o, first) for o in range(PASSES) for first in range(0, HALF, GROUP)]
             for i, (o, first) in enumerate(steps):
-                g = (h * HALF + first) // GROUP
                 nc.tensor.matmul_mx(
                     out=banks[h][:, first : first + GROUP],
                     lhsT=q_codes[o][:].bitcast(FP8X4),
                     lhsT_scale=q_scales[o][:],
                     rhs=keys[h, o][:, first : first + GROUP].bitcast(FP4X4),
-                    rhs_scale=planes[:, o, g * GROUP : (g + 1) * GROUP],
+                    rhs_scale=planes[h][:, o, first : first + GROUP],
                     start=(i == 0),
                     stop=(i == len(steps) - 1),
                 )

@@ -62,8 +62,8 @@ def tile_attend_nrm_minmax_topk_kernel(tc, qT, k_words, k_scales, offs, out):
         def list_half(h):
             return offsets[:, h * HALF // STRIPE : (h + 1) * HALF // STRIPE]
 
-        def move_scales(h, queues):
-            for j, queue in enumerate(queues):
+        def move_scales(h, queue):
+            for j in range(P // QUADRANT):
                 queue.dma_start(
                     out=planes[h][QUADRANT * j : QUADRANT * j + 4].rearrange("p o n -> p (o n)").bitcast(I32),
                     in_=picked_scales[h][8 * j : 8 * j + 8, :].bitcast(I32),
@@ -72,10 +72,10 @@ def tile_attend_nrm_minmax_topk_kernel(tc, qT, k_words, k_scales, offs, out):
         picked_scales = [sb.tile([P, HALF], U8, name=f"picked_scales{h}", align_bytes=64) for h in range(2)]
         for h in range(2):
             nc.vector.tensor_copy(picked_scales[h][:], scale_pool[:].indirect(list_half(h)))
-        move_scales(0, (nc.scalar, nc.sync, nc.scalar, nc.sync))
+        move_scales(0, nc.scalar)
         q_raw.append(sb.tile([P, PACK, NQ], F32, name="q_raw1", tag="scale_pool", align_bytes=64))
         nc.sync.dma_start(out=q_raw[1][:], in_=q_rows[1])
-        move_scales(1, (nc.scalar, nc.sync, nc.sync, nc.sync))
+        move_scales(1, nc.sync)
 
         picked = [sb.tile([P, HALF], U32, name=f"picked{h}", align_bytes=64) for h in range(2)]
         q_codes = [sb.tile([P, NQ], U32, name=f"q_codes{o}", align_bytes=64) for o in range(PASSES)]
@@ -150,7 +150,9 @@ def tile_attend_nrm_minmax_topk_kernel(tc, qT, k_words, k_scales, offs, out):
         nc.vector.tensor_scalar(flipped[:], banks[1][:], -1.0, neg_lo_first[:], ALU.mult, ALU.max, accum_out=neg_lo[:])
         nc.vector.tensor_scalar(unread[:], banks[1][:], 1.0, hi_first[:], ALU.mult, ALU.max, accum_out=hi[:])
 
-        nc.scalar.activation(above[:, 0:HALF], banks[0][:], ACT.Identity, bias=neg_lo[:], scale=1.0)
+        for first in range(0, HALF, GROUP):
+            cols = slice(first, first + GROUP)
+            nc.scalar.activation(above[:, cols], banks[0][:, cols], ACT.Identity, bias=neg_lo[:], scale=1.0)
         nc.scalar.activation(root[:], neg_lo[:], ACT.Abs_reciprocal_sqrt, bias=hi[:], scale=1.0)
         nc.vector.tensor_scalar(above[:, HALF:N], flipped[:], -1.0, neg_lo[:], ALU.mult, ALU.add)
 

@@ -32,18 +32,21 @@ def tile_attend_nrm_minmax_topk_kernel(tc, qT, k_words, k_scales, offs, out):
     nc = tc.nc
     with ExitStack() as ctx:
         sb = ctx.enter_context(tc.tile_pool(name="sb", bufs=1))
+        late = ctx.enter_context(tc.tile_pool(name="late", bufs=1))
         psum = ctx.enter_context(tc.psum_pool(name="psum", bufs=1))
 
         offsets = sb.tile([P, N // STRIPE], U16, name="offsets")
-        scale_pool = sb.tile([P, T], U8, name="scale_pool", tag="scale_pool", align_bytes=64)
-        planes = [sb.tile([P, PASSES, HALF], U8, name=f"planes{h}", align_bytes=64) for h in range(2)]
+        scale_pool = sb.tile([P, T], U8, name="scale_pool", align_bytes=64)
+        planes = sb.tile([P, PASSES, N], U8, name="planes", align_bytes=64)
         word_pool = sb.tile([P, T], I32, name="word_pool", align_bytes=64)
-        q_raw = [sb.tile([P, PACK, NQ], F32, name="q_raw0", align_bytes=64)]
+        q_raw = [
+            late.tile([P, PACK, NQ], F32, name="q_raw0", align_bytes=64, offset=2048),
+            late.tile([P, PACK, NQ], F32, name="q_raw1", align_bytes=64, offset=0),
+        ]
 
         nc.vector.memset(scale_pool[QUADRANT : 2 * QUADRANT, :].bitcast(I32), 0)
         nc.vector.memset(scale_pool[2 * QUADRANT : P, :].bitcast(I32), 0)
-        for h in range(2):
-            nc.vector.memset(planes[h][:].rearrange("p o n -> p (o n)").bitcast(I32), 0)
+        nc.vector.memset(planes[:].rearrange("p o n -> p (o n)").bitcast(I32), 0)
 
         table_in = sb.tile([P, 1], F32, name="table_in")
         table_out = sb.tile([P, 1], F32, name="table_out")
@@ -57,84 +60,96 @@ def tile_attend_nrm_minmax_topk_kernel(tc, qT, k_words, k_scales, offs, out):
         )
         nc.sync.dma_start(offsets[:], offs)
         nc.sync.dma_start(out=word_pool[:], in_=k_words[0].rearrange("p t b -> p (t b)").bitcast(I32))
-        nc.sync.dma_start(out=q_raw[0][:], in_=q_rows[0])
+        for o in range(PASSES):
+            nc.sync.dma_start(out=q_raw[o][:], in_=q_rows[o])
 
-        def list_half(h):
-            return offsets[:, h * HALF // STRIPE : (h + 1) * HALF // STRIPE]
+        def listed(slots):
+            return offsets[:, slots.start // STRIPE : slots.stop // STRIPE]
 
-        def move_scales(h, queue):
-            for j in range(P // QUADRANT):
-                queue.dma_start(
-                    out=planes[h][QUADRANT * j : QUADRANT * j + 4].rearrange("p o n -> p (o n)").bitcast(I32),
-                    in_=picked_scales[h][8 * j : 8 * j + 8, :].bitcast(I32),
-                )
+        picked_scales = sb.tile([P, N], U8, name="picked_scales", align_bytes=64)
 
-        picked_scales = [sb.tile([P, HALF], U8, name=f"picked_scales{h}", align_bytes=64) for h in range(2)]
-        for h in range(2):
-            nc.vector.tensor_copy(picked_scales[h][:], scale_pool[:].indirect(list_half(h)))
-        move_scales(0, nc.scalar)
-        q_raw.append(sb.tile([P, PACK, NQ], F32, name="q_raw1", tag="scale_pool", align_bytes=64))
-        nc.sync.dma_start(out=q_raw[1][:], in_=q_rows[1])
-        move_scales(1, nc.sync)
-
-        picked = [sb.tile([P, HALF], U32, name=f"picked{h}", align_bytes=64) for h in range(2)]
-        q_codes = [sb.tile([P, NQ], U32, name=f"q_codes{o}", align_bytes=64) for o in range(PASSES)]
-        q_scales = [sb.tile([P, NQ], U8, name=f"q_scales{o}", align_bytes=64) for o in range(PASSES)]
-        keys = {}
-
-        def part_words(h, passes, tile):
-            for i, o in enumerate(range(passes.start, passes.stop)):
-                keys[h, o] = tile[:, i]
-            nc.vector.tensor_copy(
-                tile.rearrange("p o (u n) -> p u o n", u=2),
-                picked[h][:].bitcast(U16).rearrange("p (u n o) -> p u o n", u=2, o=PASSES)[:, :, passes, :],
+        def move_scales(queue, j, slots):
+            queue.dma_start(
+                out=planes[QUADRANT * j : QUADRANT * j + 4, :, slots].bitcast(I32),
+                in_=picked_scales[8 * j : 8 * j + 8, slots].bitcast(I32),
             )
 
-        def cast(copy, o, rows, name):
-            q_grouped = sb.tile([P, PIECE, PACK], BF16, name=name, tag=name, align_bytes=64)
+        first, second, whole = slice(0, HALF), slice(HALF, N), slice(0, N)
+        for slots in (first, second):
+            nc.vector.tensor_copy(picked_scales[:, slots], scale_pool[:].indirect(listed(slots)))
+        for j, slots in ((0, first), (1, first), (2, whole), (3, whole)):
+            move_scales(nc.scalar, j, slots)
+        for j in range(2):
+            move_scales(nc.sync, j, second)
+
+        def gather_words(tile, slots):
+            nc.vector.tensor_copy(tile[:], word_pool[:].bitcast(U32).indirect(listed(slots)))
+
+        def part_words(tile, picked, o):
+            nc.vector.tensor_copy(
+                tile[:].rearrange("p (u n) -> p u n", u=2),
+                picked[:].bitcast(U16).rearrange("p (u n o) -> p o u n", u=2, o=PASSES)[:, o],
+            )
+
+        def cast(copy, tile, o, rows):
             copy(
-                q_grouped[:].rearrange("p (c i) r -> p c r i", i=4),
+                tile.rearrange("p (c i) r -> p c r i", i=4),
                 q_raw[o][:, :, rows].rearrange("p r (c i) -> p c r i", i=4),
             )
-            return q_grouped
 
-        for h in range(2):
-            nc.vector.tensor_copy(picked[h][:], word_pool[:].bitcast(U32).indirect(list_half(h)))
-        keys_first = sb.tile([P, PASSES, HALF], U16, name="keys_first", align_bytes=64)
-        part_words(0, slice(0, PASSES), keys_first[:])
+        q_codes = [sb.tile([P, NQ], U32, name=f"q_codes{o}", align_bytes=64) for o in range(PASSES)]
+        q_scales = [sb.tile([P, NQ], U8, name=f"q_scales{o}", align_bytes=64) for o in range(PASSES)]
 
-        pieces = [(o, slice(r, r + PIECE)) for o in range(PASSES) for r in range(0, NQ, PIECE)]
-        names = [f"grouped{i}" for i in range(len(pieces))]
-        copies = (nc.scalar.copy, nc.scalar.copy, nc.scalar.copy, nc.vector.tensor_copy)
-        grouped = [cast(copy, o, rows, name) for copy, (o, rows), name in zip(copies, pieces, names)]
-
-        def quantise(i):
-            o, rows = pieces[i]
+        def quantise(tile, o, rows):
             nc.vector.quantize_mx(
                 out=q_codes[o][:, rows].bitcast(FP8X4),
                 scales=q_scales[o][:, rows],
-                in_=grouped[i][:].rearrange("p w r -> p (w r)"),
+                in_=tile.rearrange("p w r -> p (w r)"),
             )
 
-        for i in range(len(pieces)):
-            quantise(i)
-        keys_last = sb.tile([P, PASSES, HALF], U16, name="keys_last", tag=names[-1], align_bytes=64)
+        picked_first = sb.tile([P, HALF], U32, name="picked_first", align_bytes=64)
+        picked_second = sb.tile([P, HALF], U32, name="picked_second", align_bytes=64)
+        keys_first = [sb.tile([P, HALF], U16, name="keys_first0", align_bytes=64)]
+        gather_words(picked_first, first)
+        gather_words(picked_second, second)
+        part_words(keys_first[0], picked_first, 0)
+
+        low, high = slice(0, PIECE), slice(PIECE, NQ)
+        grouped0 = sb.tile([P, NQ, PACK], BF16, name="grouped0", align_bytes=64)
+        grouped_low = sb.tile([P, PIECE, PACK], BF16, name="grouped_low", align_bytes=64)
+        grouped_high = sb.tile([P, PIECE, PACK], BF16, name="grouped_high", align_bytes=64)
+        cast(nc.scalar.copy, grouped0[:], 0, slice(0, NQ))
+        cast(nc.vector.tensor_copy, grouped_high[:], 1, high)
+        cast(nc.scalar.copy, grouped_low[:], 1, low)
+        quantise(grouped0[:], 0, slice(0, NQ))
+        keys_first.append(late.tile([P, HALF], U16, name="keys_first1", align_bytes=64, offset=2048))
+        part_words(keys_first[1], picked_first, 1)
+        quantise(grouped_high[:], 1, high)
+        quantise(grouped_low[:], 1, low)
+
+        keys_second = [
+            late.tile([P, HALF], U16, name=f"keys_second{o}", align_bytes=64, offset=512 * o) for o in range(PASSES)
+        ]
         for o in range(PASSES):
-            part_words(1, slice(o, o + 1), keys_last[:, o : o + 1])
+            part_words(keys_second[o], picked_second, o)
 
         banks = [psum.tile([P, HALF], F32, name=f"bank{h}") for h in range(2)]
-        for h in range(2):
-            steps = [(o, first) for o in range(PASSES) for first in range(0, HALF, GROUP)]
-            for i, (o, first) in enumerate(steps):
-                nc.tensor.matmul_mx(
-                    out=banks[h][:, first : first + GROUP],
-                    lhsT=q_codes[o][:].bitcast(FP8X4),
-                    lhsT_scale=q_scales[o][:],
-                    rhs=keys[h, o][:, first : first + GROUP].bitcast(FP4X4),
-                    rhs_scale=planes[h][:, o, first : first + GROUP],
-                    start=(i == 0),
-                    stop=(i == len(steps) - 1),
-                )
+
+        def score(target, keys, o, slots, start, stop):
+            nc.tensor.matmul_mx(
+                out=target,
+                lhsT=q_codes[o][:].bitcast(FP8X4),
+                lhsT_scale=q_scales[o][:],
+                rhs=keys.bitcast(FP4X4),
+                rhs_scale=planes[:, o, slots],
+                start=start,
+                stop=stop,
+            )
+
+        for o in range(PASSES):
+            score(banks[0][:], keys_first[o][:], o, first, o == 0, o == PASSES - 1)
+        for o in range(PASSES):
+            score(banks[1][:], keys_second[o][:], o, second, o == 0, o == PASSES - 1)
 
         flipped = sb.tile([P, HALF], F32, name="flipped")
         unread = sb.tile([P, HALF], F32, name="unread")

@@ -35,13 +35,13 @@ def tile_attend_nrm_minmax_topk_kernel(tc, qT, k_words, k_scales, offs, out):
         late = ctx.enter_context(tc.tile_pool(name="late", bufs=1))
         psum = ctx.enter_context(tc.psum_pool(name="psum", bufs=1))
 
-        offsets = sb.tile([P, N // STRIPE], U16, name="offsets")
-        scale_pool = sb.tile([P, T], U8, name="scale_pool", align_bytes=64)
-        planes = sb.tile([P, PASSES, N], U8, name="planes", align_bytes=64)
-        word_pool = sb.tile([P, T], I32, name="word_pool", align_bytes=64)
+        offsets = sb.tile([P, N // STRIPE], U16, name="offsets", align_bytes=256)
+        scale_pool = sb.tile([P, T], U8, name="scale_pool", align_bytes=256)
+        planes = sb.tile([P, PASSES, N], U8, name="planes", align_bytes=256)
+        word_pool = sb.tile([P, T], I32, name="word_pool", align_bytes=256)
         q_raw = [
-            late.tile([P, PACK, NQ], F32, name="q_raw0", align_bytes=64, offset=2048),
-            late.tile([P, PACK, NQ], F32, name="q_raw1", align_bytes=64, offset=0),
+            late.tile([P, PACK, NQ], F32, name="q_raw0", align_bytes=256, offset=2048),
+            late.tile([P, PACK, NQ], F32, name="q_raw1", align_bytes=256, offset=0),
         ]
 
         nc.vector.memset(scale_pool[QUADRANT : 2 * QUADRANT, :].bitcast(I32), 0)
@@ -66,7 +66,7 @@ def tile_attend_nrm_minmax_topk_kernel(tc, qT, k_words, k_scales, offs, out):
         def listed(slots):
             return offsets[:, slots.start // STRIPE : slots.stop // STRIPE]
 
-        picked_scales = sb.tile([P, N], U8, name="picked_scales", align_bytes=64)
+        picked_scales = sb.tile([P, N], U8, name="picked_scales", align_bytes=256)
 
         def move_scales(queue, j, slots):
             queue.dma_start(
@@ -97,8 +97,8 @@ def tile_attend_nrm_minmax_topk_kernel(tc, qT, k_words, k_scales, offs, out):
                 q_raw[o][:, :, rows].rearrange("p r (c i) -> p c r i", i=4),
             )
 
-        q_codes = [sb.tile([P, NQ], U32, name=f"q_codes{o}", align_bytes=64) for o in range(PASSES)]
-        q_scales = [sb.tile([P, NQ], U8, name=f"q_scales{o}", align_bytes=64) for o in range(PASSES)]
+        q_codes = [sb.tile([P, NQ], U32, name=f"q_codes{o}", align_bytes=256) for o in range(PASSES)]
+        q_scales = [sb.tile([P, NQ], U8, name=f"q_scales{o}", align_bytes=256) for o in range(PASSES)]
 
         def quantise(tile, o, rows):
             nc.vector.quantize_mx(
@@ -107,28 +107,28 @@ def tile_attend_nrm_minmax_topk_kernel(tc, qT, k_words, k_scales, offs, out):
                 in_=tile.rearrange("p w r -> p (w r)"),
             )
 
-        picked_first = sb.tile([P, HALF], U32, name="picked_first", align_bytes=64)
-        picked_second = sb.tile([P, HALF], U32, name="picked_second", align_bytes=64)
-        keys_first = [sb.tile([P, HALF], U16, name="keys_first0", align_bytes=64)]
+        picked_first = sb.tile([P, HALF], U32, name="picked_first", align_bytes=256)
+        picked_second = sb.tile([P, HALF], U32, name="picked_second", align_bytes=256)
+        keys_first = [sb.tile([P, HALF], U16, name="keys_first0", align_bytes=256)]
         gather_words(picked_first, first)
         gather_words(picked_second, second)
         part_words(keys_first[0], picked_first, 0)
 
         low, high = slice(0, PIECE), slice(PIECE, NQ)
-        grouped0 = sb.tile([P, NQ, PACK], BF16, name="grouped0", align_bytes=64)
-        grouped_low = sb.tile([P, PIECE, PACK], BF16, name="grouped_low", align_bytes=64)
-        grouped_high = sb.tile([P, PIECE, PACK], BF16, name="grouped_high", align_bytes=64)
+        grouped0 = sb.tile([P, NQ, PACK], BF16, name="grouped0", align_bytes=256)
+        grouped_low = sb.tile([P, PIECE, PACK], BF16, name="grouped_low", align_bytes=256)
+        grouped_high = sb.tile([P, PIECE, PACK], BF16, name="grouped_high", align_bytes=256)
         cast(nc.scalar.copy, grouped0[:], 0, slice(0, NQ))
         cast(nc.vector.tensor_copy, grouped_high[:], 1, high)
         cast(nc.scalar.copy, grouped_low[:], 1, low)
         quantise(grouped0[:], 0, slice(0, NQ))
-        keys_first.append(late.tile([P, HALF], U16, name="keys_first1", align_bytes=64, offset=2048))
+        keys_first.append(late.tile([P, HALF], U16, name="keys_first1", align_bytes=256, offset=2048))
         part_words(keys_first[1], picked_first, 1)
         quantise(grouped_high[:], 1, high)
         quantise(grouped_low[:], 1, low)
 
         keys_second = [
-            late.tile([P, HALF], U16, name=f"keys_second{o}", align_bytes=64, offset=512 * o) for o in range(PASSES)
+            late.tile([P, HALF], U16, name=f"keys_second{o}", align_bytes=256, offset=512 * o) for o in range(PASSES)
         ]
         for o in range(PASSES):
             part_words(keys_second[o], picked_second, o)
@@ -159,15 +159,13 @@ def tile_attend_nrm_minmax_topk_kernel(tc, qT, k_words, k_scales, offs, out):
         hi = sb.tile([P, 1], F32, name="hi")
         root = sb.tile([P, 1], F32, name="root")
         above = sb.tile([P, N], F32, name="above")
-        result = sb.tile([P, N], F32, name="result")
+        result = sb.tile([P, N], F32, name="result", align_bytes=256)
         nc.vector.tensor_reduce(neg_lo_first[:], banks[0][:], mybir.AxisListType.X, ALU.min, negate=True)
         nc.vector.tensor_reduce(hi_first[:], banks[0][:], mybir.AxisListType.X, ALU.max)
         nc.vector.tensor_scalar(flipped[:], banks[1][:], -1.0, neg_lo_first[:], ALU.mult, ALU.max, accum_out=neg_lo[:])
         nc.vector.tensor_scalar(unread[:], banks[1][:], 1.0, hi_first[:], ALU.mult, ALU.max, accum_out=hi[:])
 
-        for first in range(0, HALF, GROUP):
-            cols = slice(first, first + GROUP)
-            nc.scalar.activation(above[:, cols], banks[0][:, cols], ACT.Identity, bias=neg_lo[:], scale=1.0)
+        nc.scalar.activation(above[:, first], banks[0][:], ACT.Identity, bias=neg_lo[:], scale=1.0)
         nc.scalar.activation(root[:], neg_lo[:], ACT.Abs_reciprocal_sqrt, bias=hi[:], scale=1.0)
         nc.vector.tensor_scalar(above[:, HALF:N], flipped[:], -1.0, neg_lo[:], ALU.mult, ALU.add)
 

@@ -36,17 +36,17 @@ def tile_attend_nrm_minmax_topk_kernel(tc, qT, k_words, k_scales, offs, out):
         psum = ctx.enter_context(tc.psum_pool(name="psum", bufs=1))
 
         offsets = sb.tile([P, N // STRIPE], U16, name="offsets", align_bytes=256)
-        scale_pool = sb.tile([P, T], U8, name="scale_pool", align_bytes=256)
-        planes = sb.tile([P, PASSES, N], U8, name="planes", align_bytes=256)
+        scale_pool = late.tile([P, T], U8, name="scale_pool", align_bytes=256, offset=0)
+        planes = [sb.tile([P, PASSES, HALF], U8, name=f"planes{h}", align_bytes=256) for h in range(2)]
         word_pool = sb.tile([P, T], I32, name="word_pool", align_bytes=256)
         q_raw = [
             late.tile([P, PACK, NQ], F32, name="q_raw0", align_bytes=256, offset=2048),
-            late.tile([P, PACK, NQ], F32, name="q_raw1", align_bytes=256, offset=0),
         ]
 
         nc.vector.memset(scale_pool[QUADRANT : 2 * QUADRANT, :].bitcast(I32), 0)
         nc.vector.memset(scale_pool[2 * QUADRANT : P, :].bitcast(I32), 0)
-        nc.vector.memset(planes[:].rearrange("p o n -> p (o n)").bitcast(I32), 0)
+        for h in range(2):
+            nc.vector.memset(planes[h][:].rearrange("p o n -> p (o n)").bitcast(I32), 0)
 
         table_in = sb.tile([P, 1], F32, name="table_in")
         table_out = sb.tile([P, 1], F32, name="table_out")
@@ -60,27 +60,37 @@ def tile_attend_nrm_minmax_topk_kernel(tc, qT, k_words, k_scales, offs, out):
         )
         nc.sync.dma_start(offsets[:], offs)
         nc.sync.dma_start(out=word_pool[:], in_=k_words[0].rearrange("p t b -> p (t b)").bitcast(I32))
-        for o in range(PASSES):
-            nc.sync.dma_start(out=q_raw[o][:], in_=q_rows[o])
+        nc.sync.dma_start(out=q_raw[0][:], in_=q_rows[0])
 
         def listed(slots):
             return offsets[:, slots.start // STRIPE : slots.stop // STRIPE]
 
-        picked_scales = sb.tile([P, N], U8, name="picked_scales", align_bytes=256)
+        picked_scales = [sb.tile([P, HALF], U8, name=f"picked_scales{h}", align_bytes=256) for h in range(2)]
 
-        def move_scales(queue, j, slots):
+        def move_both(queue, h, j):
             queue.dma_start(
-                out=planes[QUADRANT * j : QUADRANT * j + 4, :, slots].bitcast(I32),
-                in_=picked_scales[8 * j : 8 * j + 8, slots].bitcast(I32),
+                out=planes[h][QUADRANT * j : QUADRANT * j + 4].rearrange("p o n -> p (o n)").bitcast(I32),
+                in_=picked_scales[h][8 * j : 8 * j + 8, :].bitcast(I32),
             )
 
-        first, second, whole = slice(0, HALF), slice(HALF, N), slice(0, N)
-        for slots in (first, second):
-            nc.vector.tensor_copy(picked_scales[:, slots], scale_pool[:].indirect(listed(slots)))
-        for j, slots in ((0, first), (1, first), (2, whole), (3, whole)):
-            move_scales(nc.scalar, j, slots)
-        for j in range(2):
-            move_scales(nc.sync, j, second)
+        def move_one(queue, h, j, o):
+            queue.dma_start(
+                out=planes[h][QUADRANT * j : QUADRANT * j + 4, o].bitcast(I32),
+                in_=picked_scales[h][8 * j + o : 8 * j + 8 : 2, :].bitcast(I32),
+            )
+
+        first, second = slice(0, HALF), slice(HALF, N)
+        for h, slots in enumerate((first, second)):
+            nc.vector.tensor_copy(picked_scales[h][:], scale_pool[:].indirect(listed(slots)))
+        for j in range(4):
+            move_both(nc.scalar, 0, j)
+        q_raw.append(late.tile([P, PACK, NQ], F32, name="q_raw1", align_bytes=256, offset=0))
+        nc.sync.dma_start(out=q_raw[1][:], in_=q_rows[1])
+        for j in (0, 1):
+            move_both(nc.sync, 1, j)
+        for o in range(PASSES):
+            for j in (2, 3):
+                move_one(nc.sync, 1, j, o)
 
         def gather_words(tile, slots):
             nc.vector.tensor_copy(tile[:], word_pool[:].bitcast(U32).indirect(listed(slots)))
@@ -135,21 +145,21 @@ def tile_attend_nrm_minmax_topk_kernel(tc, qT, k_words, k_scales, offs, out):
 
         banks = [psum.tile([P, HALF], F32, name=f"bank{h}") for h in range(2)]
 
-        def score(target, keys, o, slots, start, stop):
+        def score(target, keys, o, h, start, stop):
             nc.tensor.matmul_mx(
                 out=target,
                 lhsT=q_codes[o][:].bitcast(FP8X4),
                 lhsT_scale=q_scales[o][:],
                 rhs=keys.bitcast(FP4X4),
-                rhs_scale=planes[:, o, slots],
+                rhs_scale=planes[h][:, o],
                 start=start,
                 stop=stop,
             )
 
         for o in range(PASSES):
-            score(banks[0][:], keys_first[o][:], o, first, o == 0, o == PASSES - 1)
+            score(banks[0][:], keys_first[o][:], o, 0, o == 0, o == PASSES - 1)
         for o in range(PASSES):
-            score(banks[1][:], keys_second[o][:], o, second, o == 0, o == PASSES - 1)
+            score(banks[1][:], keys_second[o][:], o, 1, o == 0, o == PASSES - 1)
 
         flipped = sb.tile([P, HALF], F32, name="flipped")
         unread = sb.tile([P, HALF], F32, name="unread")

@@ -103,8 +103,8 @@ def tile_attend_nrm_minmax_topk_kernel(tc, qT, k_words, k_scales, offs, out):
 
         def cast(copy, tile, o, rows):
             copy(
-                tile.rearrange("p (c i) r -> p c r i", i=4),
-                q_raw[o][:, :, rows].rearrange("p r (c i) -> p c r i", i=4),
+                tile.rearrange("p (c i) r -> p c r i", i=2),
+                q_raw[o][:, :, rows].rearrange("p r (c i) -> p c r i", i=2),
             )
 
         q_codes = [sb.tile([P, NQ], U32, name=f"q_codes{o}", align_bytes=256) for o in range(PASSES)]

from contextlib import ExitStack

import concourse.mybir as mybir

F32 = mybir.dt.float32
BF16 = mybir.dt.bfloat16
I32 = mybir.dt.int32
U32 = mybir.dt.uint32
U16 = mybir.dt.uint16
U8 = mybir.dt.uint8
FP8X4 = mybir.dt.float8_e4m3fn_x4
FP4X4 = mybir.dt.float4_e2m1fn_x4
ALU = mybir.AluOpType
ACT = mybir.ActivationFunctionType

P = 128
QUADRANT = 32
PACK = 4
PASSES = 2
T = 2048
N = 512
NQ = 128
HALF = N // 2
GROUP = 128
PIECE = NQ // 2
STRIPE = 16

FLOPS = 2 * NQ * N * PASSES * P * PACK


def tile_attend_nrm_minmax_topk_kernel(tc, qT, k_words, k_scales, offs, out):
    nc = tc.nc
    with ExitStack() as ctx:
        sb = ctx.enter_context(tc.tile_pool(name="sb", bufs=1))
        late = ctx.enter_context(tc.tile_pool(name="late", bufs=1))
        psum = ctx.enter_context(tc.psum_pool(name="psum", bufs=1))

        offsets = sb.tile([P, N // STRIPE], U16, name="offsets", align_bytes=256)
        scale_pool = late.tile([P, T], U8, name="scale_pool", align_bytes=256, offset=0)
        planes = [sb.tile([P, PASSES, HALF], U8, name=f"planes{h}", align_bytes=256) for h in range(2)]
        word_pool = sb.tile([P, T], I32, name="word_pool", align_bytes=256)
        q_raw = [
            late.tile([P, PACK, NQ], F32, name="q_raw0", align_bytes=256, offset=2048),
        ]

        nc.vector.memset(scale_pool[QUADRANT : 2 * QUADRANT, :].bitcast(I32), 0)
        nc.vector.memset(scale_pool[2 * QUADRANT : P, :].bitcast(I32), 0)
        for h in range(2):
            nc.vector.memset(planes[h][:].rearrange("p o n -> p (o n)").bitcast(I32), 0)

        table_in = sb.tile([P, 1], F32, name="table_in")
        table_out = sb.tile([P, 1], F32, name="table_out")
        nc.vector.memset(table_in[:], 1.0)
        nc.scalar.activation(table_out[:], table_in[:], ACT.Abs_reciprocal_sqrt)

        q_rows = qT[0].rearrange("(o p r) w -> o p r w", o=PASSES, r=PACK)
        nc.sync.dma_start(
            out=scale_pool[0:QUADRANT, :].bitcast(I32),
            in_=k_scales.rearrange("o f t -> f o t").bitcast(I32),
        )
        nc.sync.dma_start(offsets[:], offs)
        nc.sync.dma_start(out=word_pool[:], in_=k_words[0].rearrange("p t b -> p (t b)").bitcast(I32))
        nc.sync.dma_start(out=q_raw[0][:], in_=q_rows[0])

        def listed(slots):
            return offsets[:, slots.start // STRIPE : slots.stop // STRIPE]

        picked_scales = [sb.tile([P, HALF], U8, name=f"picked_scales{h}", align_bytes=256) for h in range(2)]

        def move_both(queue, h, j):
            queue.dma_start(
                out=planes[h][QUADRANT * j : QUADRANT * j + 4].rearrange("p o n -> p (o n)").bitcast(I32),
                in_=picked_scales[h][8 * j : 8 * j + 8, :].bitcast(I32),
            )

        def move_one(queue, h, j, o):
            queue.dma_start(
                out=planes[h][QUADRANT * j : QUADRANT * j + 4, o].bitcast(I32),
                in_=picked_scales[h][8 * j + o : 8 * j + 8 : 2, :].bitcast(I32),
            )

        first, second = slice(0, HALF), slice(HALF, N)
        for h, slots in enumerate((first, second)):
            nc.vector.tensor_copy(picked_scales[h][:], scale_pool[:].indirect(listed(slots)))
        for j in range(4):
            move_both(nc.scalar, 0, j)
        q_raw.append(late.tile([P, PACK, NQ], F32, name="q_raw1", align_bytes=256, offset=0))
        nc.sync.dma_start(out=q_raw[1][:], in_=q_rows[1])
        for j in (0, 1):
            move_both(nc.sync, 1, j)
        for o in range(PASSES):
            for j in (2, 3):
                move_one(nc.sync, 1, j, o)

        def gather_words(tile, slots):
            nc.vector.tensor_copy(tile[:], word_pool[:].bitcast(U32).indirect(listed(slots)))

        def part_words(tile, picked, o):
            nc.vector.tensor_copy(
                tile[:].rearrange("p (u n) -> p u n", u=2),
                picked[:].bitcast(U16).rearrange("p (u n o) -> p o u n", u=2, o=PASSES)[:, o],
            )

        def cast(copy, tile, o, rows):
            copy(
                tile.rearrange("p (c i) r -> p c r i", i=2),
                q_raw[o][:, :, rows].rearrange("p r (c i) -> p c r i", i=2),
            )

        q_codes = [sb.tile([P, NQ], U32, name=f"q_codes{o}", align_bytes=256) for o in range(PASSES)]
        q_scales = [sb.tile([P, NQ], U8, name=f"q_scales{o}", align_bytes=256) for o in range(PASSES)]

        def quantise(tile, o, rows):
            nc.vector.quantize_mx(
                out=q_codes[o][:, rows].bitcast(FP8X4),
                scales=q_scales[o][:, rows],
                in_=tile.rearrange("p w r -> p (w r)"),
            )

        picked_first = sb.tile([P, HALF], U32, name="picked_first", align_bytes=256)
        picked_second = sb.tile([P, HALF], U32, name="picked_second", align_bytes=256)
        keys_first = [sb.tile([P, HALF], U16, name="keys_first0", align_bytes=256)]
        gather_words(picked_first, first)
        gather_words(picked_second, second)
        part_words(keys_first[0], picked_first, 0)

        low, high = slice(0, PIECE), slice(PIECE, NQ)
        grouped0 = sb.tile([P, NQ, PACK], BF16, name="grouped0", align_bytes=256)
        grouped_low = sb.tile([P, PIECE, PACK], BF16, name="grouped_low", align_bytes=256)
        grouped_high = sb.tile([P, PIECE, PACK], BF16, name="grouped_high", align_bytes=256)
        cast(nc.scalar.copy, grouped0[:], 0, slice(0, NQ))
        cast(nc.vector.tensor_copy, grouped_high[:], 1, high)
        cast(nc.scalar.copy, grouped_low[:], 1, low)
        quantise(grouped0[:], 0, slice(0, NQ))
        keys_first.append(late.tile([P, HALF], U16, name="keys_first1", align_bytes=256, offset=2048))
        part_words(keys_first[1], picked_first, 1)
        quantise(grouped_high[:], 1, high)
        quantise(grouped_low[:], 1, low)

        keys_second = [
            late.tile([P, HALF], U16, name=f"keys_second{o}", align_bytes=256, offset=512 * o) for o in range(PASSES)
        ]
        for o in range(PASSES):
            part_words(keys_second[o], picked_second, o)

        banks = [psum.tile([P, HALF], F32, name=f"bank{h}") for h in range(2)]

        def score(target, keys, o, h, start, stop):
            nc.tensor.matmul_mx(
                out=target,
                lhsT=q_codes[o][:].bitcast(FP8X4),
                lhsT_scale=q_scales[o][:],
                rhs=keys.bitcast(FP4X4),
                rhs_scale=planes[h][:, o],
                start=start,
                stop=stop,
            )

        for o in range(PASSES):
            score(banks[0][:], keys_first[o][:], o, 0, o == 0, o == PASSES - 1)
        for o in range(PASSES):
            score(banks[1][:], keys_second[o][:], o, 1, o == 0, o == PASSES - 1)

        flipped = sb.tile([P, HALF], F32, name="flipped")
        unread = sb.tile([P, HALF], F32, name="unread")
        neg_lo_first = sb.tile([P, 1], F32, name="neg_lo_first")
        hi_first = sb.tile([P, 1], F32, name="hi_first")
        neg_lo = sb.tile([P, 1], F32, name="neg_lo")
        hi = sb.tile([P, 1], F32, name="hi")
        root = sb.tile([P, 1], F32, name="root")
        above = sb.tile([P, N], F32, name="above")
        result = sb.tile([P, N], F32, name="result", align_bytes=256)
        nc.vector.tensor_reduce(neg_lo_first[:], banks[0][:], mybir.AxisListType.X, ALU.min, negate=True)
        nc.vector.tensor_reduce(hi_first[:], banks[0][:], mybir.AxisListType.X, ALU.max)
        nc.vector.tensor_scalar(flipped[:], banks[1][:], -1.0, neg_lo_first[:], ALU.mult, ALU.max, accum_out=neg_lo[:])
        nc.vector.tensor_scalar(unread[:], banks[1][:], 1.0, hi_first[:], ALU.mult, ALU.max, accum_out=hi[:])

        nc.scalar.activation(above[:, first], banks[0][:], ACT.Identity, bias=neg_lo[:], scale=1.0)
        nc.scalar.activation(root[:], neg_lo[:], ACT.Abs_reciprocal_sqrt, bias=hi[:], scale=1.0)
        nc.vector.tensor_scalar(above[:, HALF:N], flipped[:], -1.0, neg_lo[:], ALU.mult, ALU.add)

        nc.vector.tensor_scalar(result[:], above[:], root[:], root[:], ALU.mult, ALU.mult)
        nc.sync.dma_start(out=out[0], in_=result[:])
